import numpy as np, ml_dtypes
CORES = [24,25,26,27,28,29,30,31]
N = 8
import mx_ref
BF = ml_dtypes.bfloat16
def entries(a):
    return np.ascontiguousarray(a.T).reshape(-1)
def table(e):
    return np.ascontiguousarray(np.reshape(e, (-1, 16)).T).astype(np.int32)
def pick(q, e):
    c = np.concatenate([q[0].reshape(128, -1, 4), np.zeros((128, 1, 4), np.uint8)], axis=1); s = np.concatenate([q[1], np.ones((16, 1), np.uint8)], axis=1)
    return (np.ascontiguousarray(c[:, e].reshape(128, -1)), np.ascontiguousarray(s[:, e]))
def join(*qs):
    return (np.concatenate([q[0] for q in qs], axis=1), np.concatenate([q[1] for q in qs], axis=1))
def put(q, e, v):
    c, s = q[0].reshape(128, -1, 4).copy(), q[1].copy(); c[:, e] = v[0].reshape(128, -1, 4); s[:, e] = v[1]
    return (c.reshape(128, -1), s)
def pk(c, s):
    return (np.ascontiguousarray(c), mx_ref.live(s))
def emit(q):
    return q[0], q[1]
def decode(q):
    o = []
    for b in range(4):
        e = np.zeros((128, 128, 4), np.float32); e[np.arange(128), np.arange(128), b] = 1
        o.append(mx_ref.matmul(mx_ref.quantize(e.reshape(128, 512).astype(BF)), q))
    return np.stack(o, axis=2).reshape(128, -1)
def f(rng, *shape):
    return mx_ref.flush((rng.standard_normal(shape, dtype=np.float32) * np.exp2(rng.integers(-2, 3, shape[:-1] + (1,)))).astype(BF))
def wide(rng, *shape, cols=0):
    v = rng.standard_normal(shape, dtype=np.float32) * np.exp2(rng.integers(-12, 13, shape)).astype(np.float32)
    if cols: v *= np.repeat(np.exp2(rng.integers(-cols, cols + 1, shape[:-2] + (1, shape[-1] // 4))) * (rng.random(shape[:-2] + (1, shape[-1] // 4)) > 0.0625), 4, axis=-1).astype(np.float32)
    return mx_ref.flush(v.astype(BF))
P, F, R = 256, 32, 2
def big(v):
    v = np.array(v, np.float32)
    v[np.abs(v) < np.float32(2.0 ** -16)] = 0
    return v.astype(BF)
def share(v):
    return big(np.ascontiguousarray(v.reshape(128, N, 4 * P).transpose(1, 0, 2)))
def links(nb):
    return np.concatenate([entries(nb[r]).reshape(P, 3) for r in range(N)])
def graph(rng, ends=False):
    to, far, n = np.zeros((N * P, 3), int), [], P - (N - 1) * F
    for r in range(N):
        a, i = P * r + rng.permutation(P), 0
        while i < P:
            m = min(2 * int(rng.integers(2, 17)), P - i)
            if P - i - m < 4: m = P - i
            for k in range(2):
                c = np.roll(a[i:i + m], -k)
                to[c[0::2], k], to[c[1::2], k] = c[1::2], c[0::2]
            i += m
        if ends:
            h = rng.permutation(a[a < to[a, 0]])[:n]
            e = np.where(rng.random(n) < 0.5, h, to[h, 0])
        else: e = rng.permutation(a)[:n]
        far.append(rng.permutation(np.setdiff1d(a, e)).reshape(N - 1, F))
        for i in range(0, n, 2):
            if e[i + 1] in to[e[i], :2]:
                for j in range(0, n, 2):
                    if j != i and e[j + 1] not in to[e[i], :2] and e[i + 1] not in to[e[j], :2]:
                        e[i + 1], e[j + 1] = e[j + 1], e[i + 1]
                        break
        to[e[0::2], 2], to[e[1::2], 2] = e[1::2], e[0::2]
    for r in range(N):
        for q in range(r + 1, N):
            u, v = far[r][q - 1], far[q][r]
            to[u, 2], to[v, 2] = v, u
    return to
def inputs(rng, x, to):
    return {"x": x, "nb": np.stack([table(to[P * r:P * r + P].reshape(-1)) for r in range(N)]), "w": f(rng, N, 128, 512)}
def setup_inputs(rng):
    return inputs(rng, big(f(rng, N, 128, 4 * P)), graph(rng))
def setup_inputs_far(rng):
    to, n = graph(rng), np.arange(N * P)
    v = (1 + 0.5 * rng.random((128, N * P, 4))) * rng.choice([-1.0, 1.0], (128, N * P, 4))
    a = n[(to[:, 2] // P != n // P) & (n < to[:, 2])]
    b = to[a, 2]
    v[:, b] = np.abs(v[:, b]) * np.sign(v[:, a]) * np.where(rng.random((128, a.size, 4)) < 0.125, -1.0, 1.0)
    return inputs(rng, share(v), to)
def setup_inputs_none(rng):
    to, n, z = graph(rng, ends=True), np.arange(N * P), int(rng.integers(0, N))
    own = n // P == z
    size = np.where(own & (to[:, 2] // P == z), 0.125, 1.0)
    color = np.full(N * P, -1)
    for a in n[n < to[:, 0]]:
        both = np.array([a, to[a, 0]])
        near = color[to[both, 1:]].reshape(-1).tolist()
        color[both] = next(int(c) for c in rng.permutation(5) if c not in near)
    v = rng.choice([-1.0, 1.0], (128, N * P, 4))
    a = n[(to[:, 2] // P != n // P) & (n < to[:, 2])]
    v[:, to[a, 2]] = v[:, a]
    v[:40] = np.where((np.arange(40) // 8)[:, None, None] == color[None, :, None], 8.0, 0.0)
    v[40:48] = 64.0
    v = np.where(own[None, :, None], (1 + 0.5 * rng.random((128, N * P, 4))) * size[None, :, None], 16.0 * v)
    return inputs(rng, share(v), to)
def setup_inputs_spread(rng):
    return inputs(rng, big(wide(rng, N, 128, 4 * P, cols=6)), graph(rng))
def setup_inputs_ties(rng):
    to = graph(rng)
    t = f(rng, 128, 12).astype(np.float32).reshape(128, 3, 4)
    five = np.concatenate([t, 0 - t[:, :1], np.zeros((128, 1, 4), np.float32)], axis=1)
    e = rng.integers(0, 5, N * P)
    for r in range(N):
        j = P * r + int(rng.integers(0, P))
        e[to[j]] = 0
        e[to[to[j]].reshape(-1)] = 0
    return inputs(rng, share(five[:, e]), to)
def setup_inputs_twice(rng):
    to, large = graph(rng), np.zeros(N * P, bool)
    v = np.abs(rng.standard_normal((128, N * P, 4))) * np.exp2(rng.integers(-1, 2, (1, N * P, 1)))
    for i in range(P // 32):
        for r in rng.permutation(N):
            for j in rng.permutation(P):
                n1 = P * r + j
                n2 = to[n1, 1]
                p = np.array([to[n1, 0], n1, n2, to[n2, 0]])
                if i == 0:
                    m = to[[n1, n2], 2]
                    q = np.concatenate([p, m])
                    if large[q].any() or large[to[q]].any() or np.count_nonzero(np.isin(to[q], q)) != 10: continue
                    size = np.concatenate([rng.choice([1.0, 1.25], (128, 4, 4)), rng.choice([3.5, 4.0], (128, 2, 4))], axis=1) * 2.0 ** 26
                    v[:, q] = size * rng.choice([-1.0, 1.0], (128, 1, 4)) * np.array([1.0, 1.0, -1.0, -1.0, -1.0, 1.0])[None, :, None]
                    large[q] = True
                    large[to[m]] = True
                    break
                if large[p].any() or large[to[p]].any() or np.isin(to[p, 2], p).any() or to[p[0], 1] == p[3]: continue
                large[p] = True
                v[:, p] = (1 + 0.5 * rng.random((128, 4, 4))) * np.array([256.0, 64.0, 64.0, 256.0])[None, :, None]
                break
    return inputs(rng, share(v), to)
def check_inputs(d):
    b = []
    for k, low, high in (("x", -16, 28), ("w", -30, 30)):
        v = np.abs(d[k].astype(np.float32))
        if not (np.isfinite(v).all() and ((v == 0) | (v >= 2.0 ** low) & (v <= 2.0 ** high)).all()): b.append("a value of " + k)
    to, n = links(d["nb"]), np.arange(N * P)
    if to.min() < 0 or to.max() >= N * P: return b + ["range of nb"]
    for k in range(3):
        if (to[to[:, k], k] != n).any() or (to[:, k] == n).any(): b.append("edges k = %d are no pairs" % k)
    if (to[:, :2] // P != n[:, None] // P).any(): b.append("an edge k = 0 or 1 leaves its rank")
    if (to[:, 0] == to[:, 1]).any() or (to[:, 0] == to[:, 2]).any() or (to[:, 1] == to[:, 2]).any(): b.append("two edges of a node lead to the same node")
    c = np.zeros((N, N), int)
    np.add.at(c, (n // P, to[:, 2] // P), 1)
    if (c[~np.eye(N, dtype=bool)] != F).any(): b.append("number of edges between two ranks")
    return b
def scores(h, to):
    s = np.zeros((N * P, 3), np.float32)
    for i in range(0, N * P, 128):
        a = pick(h, np.arange(i, i + 128))
        for k in range(3): s[i:i + 128, k] = np.diagonal(mx_ref.matmul(a, pick(h, to[i:i + 128, k]))) + np.float32(0)
    return s
def reference(x, nb, w):
    to, n = links(nb), np.arange(N * P)
    h = join(*[mx_ref.quantize(np.ascontiguousarray(x[r])) for r in range(N)])
    merged, pr = np.zeros((N * P, 3), bool), np.zeros((N, R, P), np.float32)
    for t in range(R):
        s = scores(h, to)
        s[merged] = -np.inf
        c = np.argmax(s, axis=1)
        v = to[n, c]
        met = c[v] == c
        merged[n[met], c[met]] = True
        pr[:, t] = np.where(met, v, -1).reshape(N, P)
        d = decode(h).reshape(128, N * P, 4)
        m = np.float32(0.5) * d + np.float32(0.5) * d[:, np.where(met, v, n)]
        new = mx_ref.quantize(np.ascontiguousarray(m.reshape(128, -1).astype(BF)))
        h = pick(join(h, new), np.where(met, N * P + n, n))
    oc, osc, y = np.zeros((N, 128, 4 * P), np.uint8), np.zeros((N, 16, P), np.uint8), np.zeros((N, 128, P), np.float32)
    for r in range(N):
        own = pick(h, np.arange(P * r, P * r + P))
        oc[r], osc[r] = emit(own)
        y[r] = mx_ref.matmul(mx_ref.quantize(np.ascontiguousarray(w[r])), own)
    return {"oc": oc, "osc": osc, "pr": pr, "y": y}

@@ -1,0 +1,655 @@
+import math
+from concourse.bass import DstId, RemoteDMATransfer
+from concourse.mybir import dt, AluOpType, AxisListType, ActivationFunctionType
+
+OP = AluOpType
+AF = ActivationFunctionType
+BIG = 4096.0
+RND = 1.5 * 2.0 ** 28
+CY = 1.1e-3
+FP8, U8, F32, BF, I32, U16 = "float8_e4m3fn_x4", "uint8", "float32", "bfloat16", "int32", "uint16"
+ORDER = """
+32 42 5 2 6 1 0 3 56 35 4 7 14 12 43 11 31 10 46 13 18 40 16 63 60 15 33 17 37 47 166 50 65 49 34 51 48 64 38 68 87 52 9 72 69 62 58 41 53 66
+59 61 74 205 97 90 36 96 73 99 75 98 76 167 71 54 24 20 8 100 26 84 25 55 45 21 22 23 101 19 28 237 29 57 30 103 27 102 77 105 104 44 106 107
+227 70 67 109 81 108 94 127 92 110 111 114 118 129 79 113 91 112 116 165 115 39 119 93 121 120 78 89 117 209 122 156 155 131 128 123 140 157
+158 124 125 159 141 142 160 126 161 143 80 229 88 162 133 149 95 134 132 145 168 130 361 150 163 144 135 152 151 164 153 203 136 148 154 191
+146 169 214 137 82 170 228 139 171 147 173 172 187 138 181 206 178 174 185 179 176 213 177 86 186 195 384 182 183 189 188 231 175 190 184 235
+211 192 210 222 207 216 180 215 218 208 196 221 239 217 197 212 199 238 202 220 241 232 193 240 201 219 200 233 243 242 223 342 245 198 244
+346 224 204 85 83 246 230 225 194 247 276 248 226 277 280 234 278 249 250 279 257 281 251 258 282 252 236 283 256 255 284 254 285 253 264 363
+286 263 307 349 262 287 345 357 308 309 272 288 273 261 266 259 310 269 260 271 370 358 265 376 267 268 274 270 275 292 356 311 291 294 293
+313 362 289 297 312 354 343 301 355 367 359 377 316 360 302 317 295 318 303 365 314 304 298 305 315 306 336 319 320 296 368 321 364 290 331
+322 323 335 333 300 324 326 328 332 327 329 369 299 366 381 347 371 379 380 325 372 344 348 334 330 373 351 353 374 382 352 386 350 383 385
+378 388 340 387 337 390 389 338 392 391 393 430 395 434 375 394 431 432 401 341 397 433 396 339 400 435 412 398 436 411 399 437 410 409 438
+404 408 407 417 443 418 405 402 439 416 445 444 440 427 413 406 403 420 415 447 421 414 441 446 425 423 419 426 422 448 428 442 424 449 429
+457 456 461 460 459 450 464 467 463 462 451 466 468 458 452 469 453 470 454 465 455 471
+"""
+
+SCRATCH = {"nst": ("dram", [16, 138], I32)}
+for _t, _l in (
+        (F32, "t48 48 k3 48 g24 48 j64 64 g48 48 d8 8 ones 128 idn 128 sqa 128 sqb 256 gms 8 col 8 col2 4 gl48 48 own48 48 "
+              "jl 16 jw 16 dm 64 rs16 64 rs8 48 rs3 48 rs24 48 gm 48 gmt 48 mk48 48 msk 16 dw 32 iv 32 xg 64 xg2 64 hl 20 hls 8 "
+              "xl0 32 xl1 32 xlt 64 mn 256 gs 528 gg 64 sc 64 pen 20 sm 32 m0 2 m1 2 ma0 8 ma1 8 mx0 8 mx1 8 mq 128 "
+              "tkc 18 xd 260 jk 256 jq 128 z 192 zp 176 zb 80 fp 96 lnf 96 fl 144 ys 256 tab 2304"),
+        (BF, "xt 1024 wt 512 iob 256 one 516 rowb 256 rowd 128 rowc 128 kr 256 krs 256 phb 2 et 516 pa 1024 P1 584 P2 896 U0 640 U1 640 "
+             "posn 256 nr 512 nat 64 ct 2048 nt 1024"),
+        (I32, "nbw 48 nn 138 hi 48 xi 180")):
+    _w = _l.split()
+    for _n, _k in zip(_w[0::2], _w[1::2]):
+        SCRATCH[_n] = ("sbuf", [128, int(_k)], _t)
+PIECE = {}
+for _b, _t, _l in (
+        ("uu", U16, "ku 16 l18 18 o01 32 of4 4 xo 4 xoa 4 ofx 8 lp 32 ln 36 pl 16"),
+        ("cn", I32, "pp 2 ci 6"),
+        ("fa", F32, "n2m 48 xa 48 kw 48 xm 48 kf 48 ks 48 km 48 kc 48 ss 2 lo 2 ph 4 nv 4 wr 2 tkw 16")):
+    _w, _c = _l.split(), 0
+    for _n, _k in zip(_w[0::2], _w[1::2]):
+        PIECE[_n] = (_b, _c, int(_k))
+        _c += int(_k)
+    SCRATCH[_b] = ("sbuf", [128, _c], _t)
+_w = "pa 256 pm 256 pl2 256 q0 256 qw 128 b0 768 b1 512 f 512 oq 256 eq 512 cq 512 uq 512 p0 256 p1 256".split()
+for _n, _k in zip(_w[0::2], _w[1::2]):
+    SCRATCH[_n + "c"] = ("sbuf", [128, int(_k)], FP8)
+    SCRATCH[_n + "s"] = ("sbuf", [128, int(_k)], U8)
+for _k in range(8):
+    SCRATCH["bk%d" % _k] = ("psum", [128, 512], F32)
+
+SEMAPHORES = ["qv", "qs", "qt", "qp", "lnb", "lx", "lx2", "lx3", "lw", "lst", "lnn", "st0", "lm0", "lm1", "loc", "a0", "a1", "e0", "e1"]
+
+
+def program(g, core, T, topo):
+    r = T.rank_of(core)
+    blk = [(r + q) % 8 for q in range(8)]
+    lb = blk[r]
+    Q = {"v": g.vector, "s": g.scalar, "t": g.tensor, "y": g.sync, "p": g}
+    cnt = {}
+    known = {k: {} for k in Q}
+    acc = {}
+    ops = []
+    group = {}
+
+    def meet(a, b):
+        return a[0] < b[1] and b[0] < a[1] and (a[0] - b[0]) % math.gcd(a[2], b[2]) == 0
+
+    def issue(q, fn, reads, writes, sem, n, dur, lat=None):
+        deps, me = set(), len(ops)
+        for w, regs in ((False, reads), (True, writes)):
+            for b, lo, hi, st in regs:
+                for a in acc.get(b, []):
+                    if (w or a[3]) and meet((lo, hi, st), a):
+                        deps.update(group.get(ops[a[4]][3], [a[4]]))
+        ops.append([q, fn, sorted(deps), sem, n, dur, dur if lat is None else lat])
+        if n != 1:
+            group.setdefault(sem, []).append(me)
+        for w, regs in ((False, reads), (True, writes)):
+            for b, lo, hi, st in regs:
+                l = acc.setdefault(b, [])
+                if w and st == 1:
+                    l[:] = [a for a in l if not (lo <= a[0] and a[1] <= hi)]
+                l.append((lo, hi, st, w, me))
+        return me
+
+    def emit():
+        total = {m: sum(ops[i][4] for i in l) for m, l in group.items()}
+        count, clock = [0] * len(ops), [None] * len(ops)
+        for i in ([int(k) for k in ORDER.split()] or range(len(ops))):
+            q, fn, deps, sem, n = ops[i][:5]
+            if q == "a":
+                count[i], clock[i] = n, {}
+                continue
+            kn = known[q]
+            for d in sorted(deps, key=lambda d: -count[d]):
+                if not ops[d][3] or (q == "t" and ops[d][0] == "t"):
+                    continue
+                m = ops[d][3]
+                c = total.get(m, count[d])
+                if kn.get(m, 0) < c:
+                    Q[q].wait_ge(T.sem[m], c)
+                    kn[m] = c
+                for k, v in clock[d].items():
+                    kn[k] = max(kn.get(k, 0), v)
+            ins = fn()
+            if sem:
+                ins.then_inc(T.sem[sem], n)
+                cnt[sem] = cnt.get(sem, 0) + n
+                count[i] = cnt[sem]
+            clock[i] = dict(kn)
+
+    def R(n, a=0, b=None, s=1):
+        n, base, w = PIECE.get(n, (n, 0, SCRATCH[n][1][1] if n in SCRATCH else 0))
+        a, b = base + a, base + (w if b is None else b)
+        ap = T[n][:, slice(a, b) if s == 1 else slice(a, b, s)]
+        if SCRATCH[n][0] == "psum":
+            return ap, [(n, 0, 512, 1)]
+        return ap, [(n, a, b, s)]
+
+    def W32(v):
+        return v[0].bitcast(dt.uint32), v[1]
+
+    def W8(v):
+        return v[0].bitcast(dt.uint8), v[1]
+
+    def ind(win, off):
+        return win[0].indirect(off[0]), win[1] + off[1]
+
+    def val(s):
+        return (s[0], s[1]) if isinstance(s, tuple) else (s, [])
+
+    def us(n, c=1.0):
+        return max(64, n * c) * CY
+
+    def width(v):
+        r0 = v[1][0]
+        return -(-(r0[2] - r0[1]) // r0[3])
+
+    def half(*vs):
+        return 0.5 if all(SCRATCH[v[1][0][0]][2] in (BF, U16) for v in vs) else 1.0
+
+    def ts(o, i, s1, op0, s2=None, op1=None):
+        a, b = val(s1), val(s2)
+        rd = i[1] + a[1] + b[1]
+        d = (0.05 + us(width(o), 1.5)) if len(i[1]) > 1 else us(width(o), half(o, i))
+        if op1 is None:
+            issue("v", lambda: g.vector.tensor_scalar(o[0], i[0], a[0], None, op0), rd, o[1], "qv", 1, d)
+        else:
+            issue("v", lambda: g.vector.tensor_scalar(o[0], i[0], a[0], b[0], op0, op1), rd, o[1], "qv", 1, d)
+
+    def tt(o, a, b, op):
+        issue("v", lambda: g.vector.tensor_tensor(o[0], a[0], b[0], op), a[1] + b[1], o[1], "qv", 1,
+              (0.05 + us(width(o), 1.5)) if len(a[1]) > 1 else us(width(o), 1 if a[1][0][0][:2] == "bk" else 2))
+
+    def cp(o, i, n=None):
+        n = n or width(o)
+        issue("v", lambda: g.vector.tensor_copy(o[0], i[0]), i[1], o[1], "qv", 1,
+              (0.05 + us(n, 1.5)) if len(i[1]) > 1 else us(n, half(o, i)))
+
+    def fill(o, c):
+        issue("v", lambda: g.vector.memset(o[0], c), [], o[1], "qv", 1, us(width(o), half(o)))
+
+    def red(o, i):
+        issue("v", lambda: g.vector.tensor_reduce(o[0], i[0], AxisListType.X, OP.add), i[1], o[1], "qv", 1, us(width(i)))
+
+    def scan(o, a, b, op0, op1, init=0.0):
+        issue("v", lambda: g.vector.tensor_tensor_scan(o[0], a[0], b[0], init, op0, op1), a[1] + b[1], o[1], "qv", 1, us(width(o), half(o, a)))
+
+    def qz(c, s, i):
+        issue("v", lambda: g.vector.quantize_mx(c[0], s[0], i[0]), i[1], c[1] + s[1], "qv", 1, 0.02 + width(i) * 0.26e-3)
+
+    def act(o, i, f=AF.Copy, bias=None, scale=None, accum=None, lock=(), n=None):
+        kw, rd, wr = {}, list(i[1]), list(o[1]) + list(lock)
+        if bias is not None:
+            kw["bias"] = val(bias)[0]
+            rd += val(bias)[1]
+        if scale is not None:
+            kw["scale"] = val(scale)[0]
+            rd += val(scale)[1]
+        if accum is not None:
+            kw["accum_out"] = accum[0]
+            wr += accum[1]
+        n = n or width(o)
+        issue("s", lambda: g.scalar.activation(o[0], i[0], f, **kw), rd, wr, "qs", 1,
+              (0.08 + us(n, 1.5)) if len(i[1]) > 1 else 0.03 + us(n))
+
+    def mm(o, lc, ls, rc, rs, start=True, stop=True):
+        issue("t", lambda: g.tensor.matmul_mx(o[0], lc[0], ls[0], rc[0], rs[0], start, stop),
+              lc[1] + ls[1] + rc[1] + rs[1], o[1], "qt", 1, us(width(rc) + 16, 1.25))
+
+    def iota(o, pat, base, cm):
+        issue("p", lambda: g.iota(o[0], pat, base, cm, allow_small_or_imprecise_dtypes=True), [], o[1], "qp", 1, 0.13 + us(width(o), 2))
+
+    def resets(o, a, b):
+        issue("p", lambda: g.affine_select(o[0], T.ones[:, 0:a * b], [[0, a], [1, b]], OP.not_equal, 0.0, 0, 0), R("ones", 0, a * b)[1], o[1], "qp", 1,
+              0.17 + us(a * b, 2))
+
+    def pickout(o, i, base, cm):
+        issue("p", lambda: g.affine_select(o[0], i[0], [[-1, width(o)]], OP.is_equal, 0.0, base, cm), i[1], o[1], "qp", 1, 0.17 + us(width(o), 2))
+
+    def sfill(o, c):
+        act(o, R("one", 0, width(o)), AF.Copy, scale=c)
+
+    def dma(q, sem, out, i):
+        issue(q, lambda: Q[q].dma_start(out[0], i[0]), i[1], out[1], sem, 16, 0.07, 2.5)
+
+    for gr in range(8):
+        dma("ys"[gr % 2], "lnb", (T.nbw[16 * gr:16 * gr + 16, :], [("nbw", 0, 48, 1)] if gr == 0 else []), (T.nb[:, :], []))
+    dma("s", "lx", R("xt"), (T.x[:, :], []))
+    dma("s", "lx2", R("P1", 72, 520), (T.x[:, 0:448], []))
+    first = True
+    for k in range(3):
+        i = 0
+        while i < 16:
+            a, o = (3 * i + k) % 16, (3 * i + k) // 16
+            n = min((15 - a) // 3 + 1, 16 - i)
+            dma("y", "lst", (T.nst[i:i + n, 46 * k:46 * k + 46], [("nst", 0, 138, 1)] if first else []),
+                (T.nb[a:a + 3 * (n - 1) + 1:3, o:o + 46], []))
+            i, first = i + n, False
+    for gr in range(8):
+        dma("y", "lnn", (T.nn[16 * gr:16 * gr + 16, :], [("nn", 0, 138, 1)] if gr == 0 else []), (T.nst[:, :], [("nst", 0, 138, 1)]))
+    for b, lo, hi in (("P2", 256, 640), ("U0", 128, 576), ("U1", 320, 576)):
+        dma("y", "lx3", R(b, lo, hi), (T.x[:, 0:hi - lo], []))
+    dma("y", "lw", R("wt"), (T.w[:, :], []))
+    nl = [R("nn", 46 * k, 46 * k + 46, 3) for k in range(3)]
+
+    iota(R("pp", 0, 1), [[0, 1]], 0, 1)
+    iota(R("pp", 1, 2), [[0, 1]], 10, 11)
+    iota(R("k3"), [[0, 16], [1, 3]], 0, 0)
+    iota(R("t48"), [[16, 16], [0, 3]], 256 * r, 0)
+    iota(R("g24"), [[0, 2], [1, 8], [0, 3]], 0, 0)
+    iota(R("rowd"), [[0, 8], [2, 16]], 0, 0)
+    iota(R("g48"), [[0, 6], [1, 8]], 0, 0)
+    iota(R("rowb"), [[0, 16], [1, 16]], 0, 0)
+    iota(R("j64"), [[0, 4], [1, 16]], 0, 0)
+    iota(R("d8"), [[0, 2], [1, 4]], 0, 0)
+    iota(R("tab", 1792, 2304), [[1, 512]], 1792, 0)
+    fill(R("one", 0, 256), 1.0)
+    scan(R("iob"), R("one", 0, 256), R("one", 0, 256), OP.add, OP.mult, -1.0)
+    fill(R("one", 256, 516), 1.0)
+    act(R("ones"), R("one", 0, 128))
+
+    def c(k):
+        return R("ci", k, k + 1)
+
+    def col(k):
+        return R("col", k, k + 1)
+
+    def col2(k):
+        return R("col2", k, k + 1)
+    ts(c(3), R("pp", 1, 2), 15, OP.bitwise_and)
+    ts(c(4), c(3), 3, OP.mult, 2, OP.add)
+    ts(c(5), c(4), 4, OP.arith_shift_right)
+    ts(c(0), R("pp", 0, 1), 15, OP.bitwise_and)
+    ts(c(1), R("pp", 0, 1), 4, OP.arith_shift_right)
+    ts(c(2), R("pp", 0, 1), 5, OP.arith_shift_right)
+    cp(R("col", 0, 6), R("ci"))
+    ts(R("mk48"), R("k3"), col(5), OP.is_equal)
+    ts(R("gmt"), R("g24"), col(1), OP.is_equal)
+    ts(R("rs3"), R("k3"), 0.0, OP.not_equal)
+    fill(R("rs24"), 1.0)
+    fill(R("rs24", 0, 48, 24), 0.0)
+    act(R("gl48"), R("t48"), AF.Identity, bias=col(3))
+    act(R("own48"), R("gl48"), AF.Copy, bias=256.0 * (1 - r))
+    for b in range(7):
+        if b % 2:
+            act(R("tab", 256 * b, 256 * b + 256), R("iob"), AF.Copy, bias=256.0 * b)
+        else:
+            ts(R("tab", 256 * b, 256 * b + 256), R("iob"), 256.0 * b, OP.add)
+    act(R("rowc"), R("rowd"), AF.Copy, bias=-255.0)
+    act(R("tkc", 0, 16), R("iob", 0, 16), AF.Copy, bias=RND - 64.0 * r, scale=32.0)
+    ts(R("tkw"), R("iob", 0, 16), 2.0 * r, OP.is_lt, 512.0, OP.mult)
+    tt(R("tkc", 0, 16), R("tkc", 0, 16), R("tkw"), OP.add)
+    for k in range(2):
+        act(R("tkc", 16 + k, 17 + k), R("iob", 2 * r + 1 - k, 2 * r + 2 - k), AF.Copy, bias=RND, scale=32.0)
+    for h in range(2):
+        act(R("nv", 2 * h, 2 * h + 1), col(1), AF.Copy, bias=128.0 * h, scale=16.0)
+        act(R("nv", 2 * h + 1, 2 * h + 2), col(3), AF.Copy)
+    ts(R("gm"), R("g48"), col(1), OP.is_equal)
+    resets(R("rs8"), 6, 8)
+    resets(R("rs16"), 4, 16)
+    ts(R("dm"), R("j64"), col(0), OP.is_equal)
+    act(R("jl"), R("iob", 0, 16), AF.Identity, bias=col(0), scale=16.0)
+    act(R("jw"), R("jl"), AF.Copy, bias=256.0)
+    act(R("z", 2, 48, 3), R("jl"))
+    act(col2(0), col(1), AF.Copy, bias=8.0)
+    act(col2(1), col(0), AF.Copy, scale=2.0)
+    act(col2(2), col(0), AF.Copy, bias=1.0, scale=2.0)
+    sfill(R("P1", 520, 584), 0.0)
+    for h in range(2):
+        act(R("P1", 522 + 30 * h, 552 + 32 * h, 4), R("gm", 0, 8), AF.Copy, scale=64.0 * r)
+    act(R("sqa"), R("rowb", 0, 128), AF.Square, bias=col(3), scale=-1.0)
+    for e in range(4):
+        act(R("pa", 512 + e, 1024, 4), R("sqa"), AF.Relu, bias=1.0, scale=-1.0)
+    qz(R("pac", 128, 256), R("pas", 128, 256), R("pa", 512, 1024))
+
+    tt(R("n2m"), R("nbw"), R("mk48"), OP.mult)
+    ts(R("hi"), R("nbw"), 1792, OP.bitwise_and)
+    tt(R("kw"), R("n2m"), R("gl48"), OP.is_gt)
+    tt(R("xa"), R("hi"), R("own48"), OP.add)
+    tt(R("xm"), R("kw"), R("xa"), OP.mult)
+    tt(R("kf"), R("n2m"), R("xm"), OP.max)
+    tt(R("km"), R("kf"), R("gmt"), OP.mult)
+    scan(R("ks"), R("rs3"), R("kf"), OP.mult, OP.add)
+    scan(R("kc"), R("rs24"), R("km"), OP.mult, OP.add)
+    cp(R("ku"), R("ks", 2, 48, 3))
+    act(R("jk"), ind(R("tab"), R("ku")), AF.Sign, bias=R("kc", 23, 24), scale=-1.0, accum=R("ss", 0, 1))
+    ts(R("kr"), ind(R("tab"), R("ku")), R("kc", 47, 48), OP.is_lt, 2.0, OP.mult)
+    scan(R("krs"), R("kr"), R("kr"), OP.add, OP.max)
+    p2 = [R("ss", 0, 1), R("krs", 255, 256)]
+    rw = [R("rowc"), R("rowd")]
+    hi2 = [R("ph", 2, 3), R("phb", 0, 1)]
+    for h in range(2):
+        ts(R("ph", h, h + 1), p2[h], -15.0 if h else 240.0, OP.add, RND, OP.add)
+        ts(hi2[h], R("ph", h, h + 1), -RND, OP.add)
+    for e in range(4):
+        ts(R("P1", e, 72, 4), R("tkc"), R("ph", e // 2, e // 2 + 1), OP.is_equal, R("nv", e, e + 1), OP.mult)
+    qz(R("pmc", 0, 128), R("pms", 0, 128), R("P1", 0, 512))
+    for e in range(4):
+        ts(R("pa", e, 512, 4), rw[e // 2], hi2[e // 2], OP.add, p2[e // 2], OP.is_equal)
+    qz(R("pac", 0, 128), R("pas", 0, 128), R("pa", 0, 512))
+    mm(R("bk6", 0, 128), R("pac", 0, 128), R("pas", 0, 128), R("pmc", 0, 128), R("pms", 0, 128))
+    cp(R("l18"), R("bk6", 0, 18))
+    ts(R("lo", 0, 1), p2[0], 255.0, OP.add, hi2[0], OP.subtract)
+    ts(R("lo", 1, 2), p2[1], hi2[1], OP.subtract)
+    for h in range(2):
+        ts(R("wr", h, h + 1), p2[h], 257.0 + 255 * h - 64 * r, OP.is_ge, -512.0, OP.mult)
+    for h in range(2):
+        a = 520 + 34 * h
+        if h == 0:
+            act(R("P1", a, 552, 4), R("gm", 0, 8), AF.Copy, scale=hi2[0])
+        else:
+            ts(R("P1", a, 584, 4), R("gm", 0, 8), hi2[1], OP.mult)
+        act(R("P1", a + 1, 552 + 32 * h, 4), R("gm", 0, 8), AF.Copy, scale=R("lo", h, h + 1))
+        act(R("P1", 523 + 30 * h, 552 + 32 * h, 4), R("gm", 0, 8), AF.Copy, scale=R("wr", h, h + 1))
+    qz(R("pmc", 128, 256), R("pms", 128, 256), R("P1", 72, 584))
+    mm(R("bk5", 0, 128), R("pac", 128, 256), R("pas", 128, 256), R("pmc", 128, 256), R("pms", 128, 256))
+    ts(R("pl"), R("bk5", 112, 128), 0.5, OP.mult)
+    act(R("z", 98, 144, 3), R("bk5", 112, 128), AF.Copy, scale=0.5, lock=R("bk5")[1])
+    act(R("posn"), ind(R("iob"), R("pl")))
+    qz(R("q0c"), R("q0s"), R("xt"))
+
+    def pick(dc, ds, a, b, sc, ss, w0, w1, off, own=False):
+        oc, os = R(dc, a, b), R(ds, a, b)
+        if own:
+            oc, os = (oc[0], [(dc, 0, 256, 1)]), (os[0], [(ds, 0, 256, 1)])
+        cp(W32(oc), ind(W32(R(sc, w0, w1)), off), b - a)
+        act(os, ind(R(ss, w0, w1), off), n=b - a)
+
+    others = [d for d in range(1, 8)]
+    far = [d for d in others if topo.die(T.cores[r ^ d]) != topo.die(core)]
+    near = [d for d in others if d not in far]
+    lanes = {}
+    for k, l in enumerate((far, near)):
+        for n, d in enumerate(l):
+            e = topo.engines(core, T.cores[r ^ d])
+            lanes[d] = [e[4 * n + k], e[4 * n + 2 + k]]
+
+    def send(srcs, dsts, sem, regs):
+        def call():
+            tf = []
+            for d in others:
+                ad = topo.addr(T.cores[r ^ d])
+                tf.append(RemoteDMATransfer(dst_ids=[DstId(rid=ad[0], pnc=ad[1])], dma_engine_mask=sum(1 << e for e in lanes[d]),
+                                            remote_sem=T.sem[sem], src=srcs(blk[r ^ d]), dst=dsts(blk[r ^ d])))
+            g.remote_dma_fused(tf, local_sem=T.sem.loc)
+            cnt["loc"] = cnt.get("loc", 0) + 14
+        me = issue("p", call, [(b, lo, hi, 1) for b, lo, hi in regs], [], None, 1, 0.7, 0.7)
+        group.setdefault(sem, []).append(len(ops))
+        ops.append(["a", None, [me], sem, 14, 0.0, 2.5])
+
+    def arrive(sem, b, lo, hi):
+        acc.setdefault(b, []).append((lo, hi, 1, True, group[sem][0]))
+
+    def send_w(bc, bs, sem):
+        send(lambda q: T[bc][:, 256 + 32 * q:288 + 32 * q].bitcast(dt.uint8), lambda q: T[bc][:, 32 * q:32 * q + 32].bitcast(dt.uint8),
+             sem, [(bc, 256, 512)])
+        send(lambda q: T[bs][:, 256 + 32 * q:288 + 32 * q], lambda q: T[bs][:, 32 * q:32 * q + 32], sem, [(bs, 256, 512)])
+
+    def bank(k, n, a=0):
+        return R("bk%d" % k, a, a + n)
+
+    def gram(bc, bs, mc, ms, m0):
+        mm(bank(0, 256), R(bc, 256, 384), R(bs, 256, 384), R(mc, m0, m0 + 256), R(ms, m0, m0 + 256))
+        for k, j in enumerate((1, 3)):
+            a = m0 + 128 * k
+            mm(bank(j, 128), R(bc, 384, 512), R(bs, 384, 512), R(mc, a, a + 128), R(ms, a, a + 128))
+        act(R("gs", 0, 256), bank(0, 256))
+        cp(R("gs", 264, 392), bank(1, 128))
+        cp(R("gs", 392, 520), bank(3, 128))
+
+    BK = [[0, 4, 5, 6], [0, 1, 2, 3]]
+
+    def dec(h, b, cc, cs, a, start):
+        w = 256 if b == 0 else 128
+        mm(bank(BK[h][b], w), R("eqc", 128 * b, 128 * b + 128), R("eqs", 128 * b, 128 * b + 128),
+           R(cc, a + 128 * h, a + 128 * h + w), R(cs, a + 128 * h, a + 128 * h + w), start, not start)
+
+    def diagonal(o, x, i, off):
+        tt(x, ind(i, off), R("dm"), OP.mult)
+        scan(o, R("rs16"), x, OP.mult, OP.add)
+
+    def local_scores(t):
+        for h in range(2):
+            tt(R("gg", 32 * h, 32 * h + 32), ind(R("gs", 264 * h, 264 * h + 264), R("xoa" if t else "xo", 2 * h, 2 * h + 2)), R("dm", 0, 32), OP.mult)
+        scan(R("sc"), R("rs16"), R("gg"), OP.mult, OP.add)
+        s0, s1 = R("sc", 15, 64, 32), R("sc", 31, 64, 32)
+        m, ma, mx = "m%d" % t, "ma%d" % t, "mx%d" % t
+        for h in range(2):
+            ts(R(ma, 4 * h, 4 * h + 4), R("msk", 4 * h, 4 * h + 4), R("sc", 15 + 32 * h, 16 + 32 * h), OP.max, R("sc", 31 + 32 * h, 32 + 32 * h), OP.max)
+        send(lambda q: T[ma][:, q:q + 1], lambda q: T[mx][:, q:q + 1], "e%d" % t, [(ma, 0, 8)])
+        b = 32 * (lb % 4)
+        rest = [(0, b), (b + 32, 128)] if 0 < b < 96 else [(32 - b // 3, 64), (64, 128 - b // 3)]
+        for i, (lo, hi, to) in enumerate([(b, b + 16, b + 16), (b + 16, b + 32, b)] + [(lo, hi, lo) for lo, hi in rest]):
+            dma("y", "lm%d" % t, (T[mx][to:to + hi - lo, lb:lb + 1], [(mx, 0, 8, 1)] if i == 0 else []), (T[ma][lo:hi, lb:lb + 1], [(ma, 0, 8, 1)]))
+        tt(R(m), s0, s1, OP.max)
+        tt(R("sm", 0, 2), s0, s1, OP.is_ge)
+        act(R("sm", 2, 6, 2), R("sm", 0, 2), AF.Copy, bias=-4e29, scale=4e29)
+        act(R("sm", 3, 6, 2), R("sm", 0, 2), AF.Copy, scale=-4e29)
+        tt(R("sm", 8, 12), R("sc", 15, 64, 16), R("sm", 2, 6), OP.add)
+
+    def statics(t, hi_own, hl):
+        for h in range(2):
+            a = 128 * t + 64 * h
+            act(R("mn", a, a + 64, 2), R("j64", 0, 32), AF.Square, bias=hi_own[h], scale=-1.0)
+            for k in range(2):
+                act(R("mn", a + 32 * k + 1, a + 32 * k + 32, 2), R("j64", 0, 16), AF.Square, bias=R("hl", hl + 2 * h + k, hl + 2 * h + k + 1), scale=-1.0)
+            act(R("nat", 32 * t + 16 * h, 32 * t + 16 * h + 16), R("mn", a, a + 32, 2), AF.Relu, bias=0.0625, scale=-0.0625)
+        for h in range(2):
+            for k in range(2):
+                a = 64 * h + 32 * k
+                act(R("mq", a, a + 32), R("mn", 128 * t + a, 128 * t + a + 32), AF.Identity,
+                    bias=R("sm", 8 + 2 * h + k, 9 + 2 * h + k), scale=-8e29)
+
+    def weights(t, lo_own, hl):
+        if t == 0:
+            act(R("sqb"), R("rowb"), AF.Square, bias=col(0), scale=-1.0)
+        for h in range(2):
+            if t == 0:
+                act(R("ct", h, 1024, 4), R("sqb"), AF.Relu, bias=BIG, scale=-BIG)
+            else:
+                ts(R("ct", 1024 * t + h, 1024 * t + 1024, 4), R("rowb"), lo_own[h], OP.is_equal, BIG, OP.mult)
+            for k in range(2):
+                a = 1024 * t + 512 * k
+                ts(R("ct", a + 2 + h, a + 512, 4), R("rowb", 0, 128), R("hl", hl + 2 * h + k, hl + 1 + 2 * h + k), OP.is_equal, BIG, OP.mult)
+        qz(R("cqc", 256 * t, 256 * t + 256), R("cqs", 256 * t, 256 * t + 256), R("ct", 1024 * t, 1024 * t + 1024))
+
+    def flags_times(t, k, b, qc, qs, uq):
+        ca = 256 * t + 128 * k
+        mm(bank(b, 128), R("cqc", ca, ca + 128), R("cqs", ca, ca + 128), R(qc, uq, uq + 128), R(qs, uq, uq + 128))
+
+    def choose(t, bc, bs):
+        u, uq, z, xl = "U%d" % t, 128 * t, 96 * t, "xl%d" % t
+        arrive("a%d" % t, bc, 0, 256)
+        arrive("a%d" % t, bs, 0, 256)
+        for h in range(2):
+            mm(bank(2 + h, 128), R(bc, 256 + 128 * h, 384 + 128 * h), R(bs, 256 + 128 * h, 384 + 128 * h),
+               R(bc, 128 * h, 128 * h + 128), R(bs, 128 * h, 128 * h + 128))
+        for h in range(2):
+            tt(R("xd", 129 * h, 129 * h + 128), bank(2 + h, 128), R("idn"), OP.mult)
+        act(R("jk", 0, 128 + t), R("xd", 0, 128 + t), AF.Identity, accum=R("sm", 16, 17))
+        red(R("sm", 17, 18), R("xd", 129, 257 + t))
+        for h in range(2):
+            ts(R(u, h, 128, 2), R("mq", 64 * h, 64 * h + 64), R("sm", 16 + h, 17 + h), OP.is_ge)
+        qz(R("uqc", uq, uq + 128), R("uqs", uq, uq + 128), R(u, 0, 512))
+        for k in range(2):
+            flags_times(t, k, 2 + k, "uqc", "uqs", uq)
+        for k in range(2):
+            tt(R("z", z + k, z + 48, 3), bank(2 + k, 16, 16 * k), R(xl, 16 * k, 16 * k + 16), OP.add)
+        scan(R("z", z + 48, z + 96), R("rs3"), R("z", z, z + 48), OP.mult, OP.max)
+        cp(R("lp", 16 * t, 16 * t + 16), R("z", z + 50, z + 96, 3))
+
+    def decide(t):
+        mx, u = "mx%d" % t, "U%d" % t
+        arrive("e%d" % t, mx, 0, 8)
+        for h in range(2):
+            ts(R("ofx", 4 * h, 4 * h + 4), R(mx, 4 * h, 4 * h + 4), R("sm", 16 + h, 17 + h), OP.is_lt, col2(1), OP.add)
+        for h in range(2):
+            act(R("jq", 64 * h, 64 * h + 64), ind(R("dw"), R("ofx", 4 * h, 4 * h + 4)), AF.Copy, accum=R("sm", 20 + h, 21 + h))
+        tt(R("sm", 22, 24), R("sm", 16, 18), R("m%d" % t), OP.is_gt)
+        for h in range(2):
+            ts(R(u, 576 + h, 640, 4), R("nat", 32 * t + 16 * h, 32 * t + 16 * h + 16), R("sm", 20 + h, 21 + h), OP.mult, R("sm", 22 + h, 23 + h), OP.mult)
+        vq = 256 + 128 * t
+        qz(R("uqc", vq, vq + 128), R("uqs", vq, vq + 128), R(u, 128, 640))
+        flags_times(t, 0, 7, "uqc", "uqs", vq)
+        a = 48 * t
+        ts(R("lnf", a, a + 16), R("z", 96 * t + 50, 96 * t + 96, 3), 256.0, OP.is_ge, 256.0, OP.mult)
+        tt(R("lnf", a + 16, a + 32), R("lnf", a, a + 16), R("jl" if t else "jw"), OP.add)
+        tt(R("lnf", a + 32, a + 48), bank(7, 16, 112), R("lnf", a + 16, a + 32), OP.add)
+        cp(R("ln", 20 * t, 20 * t + 16), R("lnf", a + 32, a + 48))
+
+    def own_parts(cc, cs, a):
+        for h, b in ((0, 0), (0, 1), (0, 2), (0, 3), (1, 1)):
+            dec(h, b, cc, cs, a, True)
+
+    def merge(t, bc, bs, cc, cs, own, base):
+        pc, psn, off = "p%dc" % t, "p%ds" % t, 16 * t
+        for h in range(2):
+            pick(pc, psn, 128 * h, 128 * h + 128, bc, bs, 0, 512, R("lp", off + 8 * h, off + 8 * h + 8))
+        for b in range(2, 4):
+            dec(1, b, cc, cs, own, True)
+        for h, b in ((0, 1), (0, 2), (0, 3), (0, 0), (1, 1), (1, 2), (1, 3)):
+            dec(h, b, pc, psn, 0, False)
+        for h in range(2):
+            for b in range(4):
+                oo = R("nt", 512 * h + b, 512 * h + 512, 4)
+                if b == 0:
+                    ts(oo, R("bk0", 128 * h, 128 * h + 128), 0.5, OP.mult)
+                elif b == 2:
+                    ts(oo, bank(BK[h][b], 128), 0.5, OP.mult)
+                else:
+                    act(oo, bank(BK[h][b], 128), AF.Copy, scale=0.5)
+            qz(R(cc, base + 128 * h, base + 128 * h + 128), R(cs, base + 128 * h, base + 128 * h + 128), R("nt", 512 * h, 512 * h + 512))
+
+    def own_block(bc, bs, sc, ss, w, off):
+        pick(bc, bs, 32 * lb, 32 * lb + 32, sc, ss, 0, w, off, True)
+
+    pick("b0c", "b0s", 256, 512, "q0c", "q0s", 0, 256, R("l18", 0, 16))
+    send_w("b0c", "b0s", "a0")
+    own_block("b0c", "b0s", "q0c", "q0s", 256, R("l18", 16, 18))
+    gram("b0c", "b0s", "q0c", "q0s", 0)
+    for k in range(2):
+        ts(R("o01", 16 * k, 16 * k + 16), nl[k], -256.0 * r, OP.add)
+    act(R("nr"), ind(R("iob"), R("o01")))
+    tt(R("iv", 0, 16), R("bk6", 0, 16), R("gm", 0, 16), OP.mult)
+    scan(R("iv", 16, 32), R("rs8", 0, 16), R("iv", 0, 16), OP.mult, OP.add)
+    inv = R("iv", 23, 32, 8)
+    cp(R("of4", 0, 4, 2), inv)
+    ts(R("of4", 1, 4, 2), inv, 256.0, OP.add)
+    diagonal(R("xi", 0, 64), R("xg"), R("nr"), R("of4"))
+    cp(R("xo"), R("xi", 15, 64, 16))
+    for h in range(2):
+        sfill(R("gs", 256 + 264 * h, 264 + 264 * h), -1e29)
+    ts(R("msk", 8, 16), R("d8"), col(2), OP.not_equal, 2e29, OP.mult)
+    ts(R("msk", 0, 8), R("msk", 8, 16), -1e29, OP.add)
+    local_scores(0)
+    diagonal(R("xi", 64, 128), R("xg2"), R("posn"), R("xo"))
+    cp(R("xi", 143, 160, 16), inv)
+    ts(R("xi", 160, 170), R("xi", 15, 160, 16), 4, OP.arith_shift_right)
+    ts(R("xi", 170, 180), R("xi", 15, 160, 16), 15, OP.bitwise_and)
+    cp(R("hl"), R("xi", 160, 180))
+    statics(0, [col(1), col2(0)], 4)
+    pickout(R("idn"), R("ones"), 0, 1)
+    ts(R("dw"), R("iob", 0, 32), col2(2), OP.is_equal)
+    weights(0, [col(0), col(0)], 14)
+    fill(R("P2", 0, 256), 0.0)
+    act(R("gms"), R("gm", 0, 8), AF.Copy, scale=1.0 / BIG)
+    for k in range(2):
+        for h in range(2):
+            a = 64 * k + 33 * h
+            ts(R("P2", a, 64 * k + 32 * h + 32, 4), R("gm", 0, 8), R("hl", 4 + 2 * h + k, 5 + 2 * h + k), OP.mult, 16.0 / BIG, OP.mult)
+            act(R("P2", a + 128, 64 * k + 32 * h + 160, 4), R("gms"), AF.Copy, scale=R("hl", 14 + 2 * h + k, 15 + 2 * h + k))
+    qz(R("pl2c", 0, 128), R("pl2s", 0, 128), R("P2", 0, 512))
+    flags_times(0, 0, 7, "pl2c", "pl2s", 0)
+    act(R("xlt", 0, 32), bank(7, 32, 32), AF.Copy, bias=256.0 - 2 * BIG)
+    tt(R("xl0"), bank(7, 32), R("xlt", 0, 32), OP.add)
+    pickout(R("et"), R("one"), 3, 4)
+    for b in range(4):
+        qz(R("eqc", 128 * b, 128 * b + 128), R("eqs", 128 * b, 128 * b + 128), R("et", 3 - b, 515 - b))
+    own_parts("b0c", "b0s", 256)
+    fill(R("U0", 576, 640), 0.0)
+    choose(0, "b0c", "b0s")
+    merge(0, "b0c", "b0s", "b0c", "b0s", 256, 512)
+    decide(0)
+    for k in range(2):
+        cp(R("ln", 16 + k, 17 + k), R("lnf", 33 + 2 * lb - k, 34 + 2 * lb - k))
+    for h in range(2):
+        pick("b1c", "b1s", 256 + 128 * h, 384 + 128 * h, "b0c", "b0s", 0, 640 + 128 * h, R("ln", 8 * h, 8 * h + 8))
+
+    send_w("b1c", "b1s", "a1")
+    own_block("b1c", "b1s", "b0c", "b0s", 768, R("ln", 16, 18))
+    gram("b1c", "b1s", "b1c", "b1s", 256)
+    for k in range(2):
+        act(R("fl", 16 * k, 16 * k + 16), R("z", k, 48, 3), AF.Sign, bias=-255.5)
+    ts(R("fl", 32, 48), bank(7, 16, 112), 128.0, OP.is_ge)
+    tt(R("fl", 48, 96), R("fl", 0, 48), R("gm"), OP.mult)
+    scan(R("fl", 96, 144), R("rs8"), R("fl", 48, 96), OP.mult, OP.add)
+    for k in range(2):
+        act(R("pen", k, 4, 2), R("fl", 103 + 16 * k, 112 + 16 * k, 8), AF.Copy, bias=128.0, scale=128.0)
+    tt(R("pen", 8, 12), R("pen", 0, 4), R("xi", 79, 128, 16), OP.max)
+    cp(R("xoa"), R("pen", 8, 12))
+    act(R("xd", 128, 258, 129), R("fl", 135, 144, 8), AF.Copy, scale=-1e29)
+    act(R("pen", 12, 16), R("fl", 103, 128, 8), AF.Copy, bias=16.0, scale=16.0)
+    act(R("pen", 16, 18), R("fl", 135, 144, 8), AF.Copy, scale=32.0)
+    local_scores(1)
+    pick("fc", "fs", 0, 256, "b1c", "b1s", 256, 512, R("pl"))
+    own_parts("fc", "fs", 0)
+    statics(1, [R("hl", 8, 9), R("hl", 9, 10)], 0)
+    weights(1, [R("hl", 18, 19), R("hl", 19, 20)], 10)
+    fill(R("P2", 640, 896), 0.0)
+    act(R("hls", 0, 4), R("hl", 4, 8), AF.Copy, scale=1.0 / 16)
+    act(R("hls", 4, 8), R("hl", 14, 18), AF.Copy, scale=1.0 / 256)
+    for e in range(2):
+        for k in range(2):
+            for h in range(2):
+                a = 640 + 128 * e + 64 * k
+                act(R("P2", a + h, a + 64, 4), R("nat", 32 + 16 * h, 48 + 16 * h), AF.Copy, scale=R("hls", 4 * e + 2 * h + k, 4 * e + 2 * h + k + 1))
+    qz(R("pl2c", 128, 256), R("pl2s", 128, 256), R("P2", 384, 896))
+    flags_times(1, 0, 7, "pl2c", "pl2s", 128)
+    act(R("xlt", 32, 64), bank(7, 32, 96), AF.Copy, bias=256.0 - 2 * BIG)
+    tt(R("xl1"), bank(7, 32, 64), R("xlt", 32, 64), OP.add)
+    fill(R("U1", 128, 320), 0.0)
+    sfill(R("U1", 576, 640), 0.0)
+    for k in range(3):
+        for h in range(2):
+            a = 128 + 64 * k
+            act(R("U1", a + h, a + 64, 4), R("nat", 32 + 16 * h, 48 + 16 * h), AF.Copy, scale=R("pen", 12 + 2 * k + h, 13 + 2 * k + h))
+    qz(R("qwc"), R("qws"), R("wt"))
+    choose(1, "b1c", "b1s")
+    cp(R("zb", 0, 16), bank(2, 16))
+    cp(R("zb", 16, 80), bank(3, 64, 16))
+    for k in (0, 1, 3, 4, 5):
+        a = 16 * k - (16 if k > 2 else 0)
+        tt(R("zp", 16 * k, 16 * k + 16), R("zb", a, a + 16), nl[k % 3], OP.add)
+    merge(1, "b1c", "b1s", "fc", "fs", 0, 256)
+    decide(1)
+    ts(R("zp", 160, 176), bank(7, 16, 112), 32.0, OP.mult)
+    tt(R("zp", 32, 48), R("zp", 160, 176), nl[2], OP.add)
+    for t in range(2):
+        a = 48 - 48 * t
+        tt(R("zp", 128 + 16 * t, 144 + 16 * t), R("zp", a, a + 16), R("zp", a + 16, a + 32), OP.max)
+        tt(R("zp", 96 + 16 * t, 112 + 16 * t), R("zp", 128 + 16 * t, 144 + 16 * t), R("zp", a + 32, a + 48), OP.max)
+    ts(R("fp", 0, 32), R("zp", 96, 128), -2 * BIG, OP.add, -1.0, OP.max)
+    tt(R("fp", 32, 64), R("fp", 0, 32), R("gm", 0, 32), OP.mult)
+    scan(R("fp", 64, 96), R("rs8", 0, 32), R("fp", 32, 64), OP.mult, OP.add)
+    for t in range(2):
+        for h in range(2):
+            a = 64 + 8 * (2 * t + h) + 7
+            dma("y", "st0", (T.pr[t:t + 1, 128 * h:128 * h + 128], []), R("fp", a, a + 1))
+    for h in range(2):
+        a, b = 128 * h, 128 * h + 128
+        pick("oqc", "oqs", a, b, "fc", "fs", 0, 384 + 128 * h, R("ln", 20 + 8 * h, 28 + 8 * h))
+        dma("y", "st0", (T.oc[:, 4 * a:4 * b], []), W8(R("oqc", a, b)))
+        mm(bank(4 + h, 128), R("qwc"), R("qws"), R("oqc", a, b), R("oqs", a, b))
+    for k in range(4):
+        dma("s" if k % 2 else "y", "st0", (T.osc[4 * k:4 * k + 4, :], []), (T.oqs[32 * k:32 * k + 4, :], [("oqs", 0, 256, 1)]))
+    cp(R("ys", 0, 128), bank(4, 128))
+    act(R("ys", 128, 256), bank(5, 128))
+    for h in range(2):
+        dma("y" if h == 0 else "s", "st0", (T.y[:, 128 * h:128 * h + 128], []), R("ys", 128 * h, 128 * h + 128))
+
+    emit()
+    cnt.update({"a0": 28, "a1": 28, "e0": 14, "e1": 14})
+    for sem in sorted(cnt):
+        g.wait_ge(T.sem[sem], cnt[sem])
+
+
+def rank_program(g, core, T, topo):
+    if T.rank_of(core) is not None:
+        program(g, core, T, topo)

@@ -6,47 +6,38 @@ OP = AluOpType
 AF = ActivationFunctionType
 BIG = 4096.0
 RND = 1.5 * 2.0 ** 28
-CY = 1.1e-3
 FP8, U8, F32, BF, I32, U16 = "float8_e4m3fn_x4", "uint8", "float32", "bfloat16", "int32", "uint16"
 ORDER = """
-32 42 5 2 6 1 0 3 56 35 4 7 14 12 43 11 31 10 46 13 18 40 16 63 60 15 33 17 37 47 166 50 65 49 34 51 48 64 38 68 87 52 9 72 69 62 58 41 53 66
-59 61 74 205 97 90 36 96 73 99 75 98 76 167 71 54 24 20 8 100 26 84 25 55 45 21 22 23 101 19 28 237 29 57 30 103 27 102 77 105 104 44 106 107
-227 70 67 109 81 108 94 127 92 110 111 114 118 129 79 113 91 112 116 165 115 39 119 93 121 120 78 89 117 209 122 156 155 131 128 123 140 157
-158 124 125 159 141 142 160 126 161 143 80 229 88 162 133 149 95 134 132 145 168 130 361 150 163 144 135 152 151 164 153 203 136 148 154 191
-146 169 214 137 82 170 228 139 171 147 173 172 187 138 181 206 178 174 185 179 176 213 177 86 186 195 384 182 183 189 188 231 175 190 184 235
-211 192 210 222 207 216 180 215 218 208 196 221 239 217 197 212 199 238 202 220 241 232 193 240 201 219 200 233 243 242 223 342 245 198 244
-346 224 204 85 83 246 230 225 194 247 276 248 226 277 280 234 278 249 250 279 257 281 251 258 282 252 236 283 256 255 284 254 285 253 264 363
-286 263 307 349 262 287 345 357 308 309 272 288 273 261 266 259 310 269 260 271 370 358 265 376 267 268 274 270 275 292 356 311 291 294 293
-313 362 289 297 312 354 343 301 355 367 359 377 316 360 302 317 295 318 303 365 314 304 298 305 315 306 336 319 320 296 368 321 364 290 331
-322 323 335 333 300 324 326 328 332 327 329 369 299 366 381 347 371 379 380 325 372 344 348 334 330 373 351 353 374 382 352 386 350 383 385
-378 388 340 387 337 390 389 338 392 391 393 430 395 434 375 394 431 432 401 341 397 433 396 339 400 435 412 398 436 411 399 437 410 409 438
-404 408 407 417 443 418 405 402 439 416 445 444 440 427 413 406 403 420 415 447 421 414 441 446 425 423 419 426 422 448 428 442 424 449 429
-457 456 461 460 459 450 464 467 463 462 451 466 468 458 452 469 453 470 454 465 455 471
+2 4 5 30 0 3 7 6 29 42 46 1 43 48 49 14 50 47 55 31 51 32 190 9 33 8 34 64 52 11 12 59 15 62 63 65 155 80 79 82 13 81 74 60 83 17 61 75 72 84 44 68 16 86 85 76 35 38 18 19 22 71 20 26 88 36 87 25 222 69 67 70 66 78 108 24 90 73 89 92 91 77 93 154 96 39 109 94 97 45 112 140 110 102 117 201 113 101 95 98 99 103 111 104 206 100 188 105 118 121 122 119 21 116 124 115 120 37 125 123 139 141 27 23 144 28 53 106 107 132 143 146 145 56 137 221 147 126 114 131 127 128 149 135 156 216 158 142 130 157 148 136 224 150 159 226 151 133 200 10 223 217 152 239 215 218 198 181 189 160 182 58 161 205 208 184 153 162 185 41 191 164 204 202 165 192 219 193 187 186 138 172 214 220 170 129 237 236 40 197 134 211 194 228 203 227 245 331 225 195 246 247 163 166 240 196 241 253 242 169 229 173 54 199 234 254 230 248 243 232 171 168 167 277 278 249 244 280 231 238 250 233 57 279 235 251 281 282 330 252 255 209 259 283 258 257 284 265 264 256 260 175 207 210 212 285 261 174 263 329 274 273 268 286 287 297 262 300 267 272 266 269 270 271 275 296 289 276 291 294 295 288 290 176 213 302 309 310 301 183 298 299 307 303 177 332 305 179 178 304 308 312 292 293 325 311 313 315 316 321 323 324 334 320 180 333 306 314 322 326 335 338 344 327 340 351 352 337 346 347 342 353 360 319 343 339 336 359 354 341 317 348 349 318 386 383 345 355 350 356 357 387 388 384 385 389 390 358 364 362 328 365 391 361 402 403 372 404 405 392 393 371 363 366 374 368 367 375 406 370 379 380 369 376 373 381 378 382 377 398 399 400 395 410 407 409 394 408 396 401 413 414 397 411 412
+"""
+ON = """
+0 1 2 6 7 8 9 10 11 12 15 16 17 18 19 20 21 22 23 24 25 26 27 28 30 31 32 33 34 35 36 37 38 39 40 41 42 43 44 45 46 47 48 49 50 51 52 53 54 56 57 58 60 61 62 64 65 66 68 69 71 72 73 74 75 76 77 80 82 83
 """
 
 SCRATCH = {"nst": ("dram", [16, 138], I32)}
 for _t, _l in (
-        (F32, "t48 48 k3 48 g24 48 j64 64 g48 48 d8 8 ones 128 idn 128 sqa 128 sqb 256 gms 8 col 8 col2 4 gl48 48 own48 48 "
-              "jl 16 jw 16 dm 64 rs16 64 rs8 48 rs3 48 rs24 48 gm 48 gmt 48 mk48 48 msk 16 dw 32 iv 32 xg 64 xg2 64 hl 20 hls 8 "
-              "xl0 32 xl1 32 xlt 64 mn 256 gs 528 gg 64 sc 64 pen 20 sm 32 m0 2 m1 2 ma0 8 ma1 8 mx0 8 mx1 8 mq 128 "
-              "tkc 18 xd 260 jk 256 jq 128 z 192 zp 176 zb 80 fp 96 lnf 96 fl 144 ys 256 tab 2304"),
-        (BF, "xt 1024 wt 512 iob 256 one 516 rowb 256 rowd 128 rowc 128 kr 256 krs 256 phb 2 et 516 pa 1024 P1 584 P2 896 U0 640 U1 640 "
-             "posn 256 nr 512 nat 64 ct 2048 nt 1024"),
-        (I32, "nbw 48 nn 138 hi 48 xi 180")):
+        (F32, "t48 48 k3 48 g24 48 j64 64 d8 8 ones 128 idn 128 col 12 gl48 48 own48 48 "
+              "jl 16 plf 16 dm 64 rs16 64 rs8 16 rs3 48 rs24 48 rs17 68 rs4 128 gmt 48 mk48 48 msk 8 dw 32 iv 32 xg 64 xg2 64 hl 32 hv 4 dif 16 dl 4 s4 4 sqa 128 "
+              "sel0 16 sel1 16 st 16 gm2 32 gd 32 c4 64 plx0 64 plx1 64 nlx 64 gs 512 gg 68 sc 68 sm 32 ma0 8 ma1 8 mx0 8 mx1 8 "
+              "tkc 18 xd 260 jk 260 jq 128 z 64 zs 64 zp 128 zq 128 tp 32 fl 32 ys 256 tab 2304"),
+        (BF, "xt 1024 wt 512 iob 256 one 516 rowb 128 rowd 128 rowc 128 kr 256 krs 256 phb 2 et 516 pa 1024 P1 768 U1 512 UC 512 "
+             "posn 256 nr 512 qn 64 qm 64 ns0 256 ns1 256 ct0 512 ct1 512 nt 1024"),
+        (I32, "nbw 48 nn 138 hi 48 xi 160")):
     _w = _l.split()
     for _n, _k in zip(_w[0::2], _w[1::2]):
         SCRATCH[_n] = ("sbuf", [128, int(_k)], _t)
 PIECE = {}
 for _b, _t, _l in (
-        ("uu", U16, "ku 16 l18 18 o01 32 of4 4 xo 4 xoa 4 ofx 8 lp 32 ln 36 pl 16"),
-        ("cn", I32, "pp 2 ci 6"),
-        ("fa", F32, "n2m 48 xa 48 kw 48 xm 48 kf 48 ks 48 km 48 kc 48 ss 2 lo 2 ph 4 nv 4 wr 2 tkw 16")):
+        ("uu", U16, "ku 16 l18 18 o01 32 of4 4 xo 4 xp 4 ofx 8 lp 32 ln 36 pl 16 cof 2 rep 4"),
+        ("cn", I32, "pp 4 ci 12"),
+        ("fa", F32, "n2m 48 xa 48 kw 48 xm 48 kf 48 ks 48 km 48 kc 48 ss 2 ph 4 tkw 16 lo 2 wr 2"),
+        ("fb", F32, "m0 2 m1 2 col2 2 c44 4 gth 16")):
     _w, _c = _l.split(), 0
     for _n, _k in zip(_w[0::2], _w[1::2]):
         PIECE[_n] = (_b, _c, int(_k))
         _c += int(_k)
     SCRATCH[_b] = ("sbuf", [128, _c], _t)
-_w = "pa 256 pm 256 pl2 256 q0 256 qw 128 b0 768 b1 512 f 512 oq 256 eq 512 cq 512 uq 512 p0 256 p1 256".split()
+_w = "pa 256 pm 256 q0 256 qw 128 b0 768 b1 768 oq 256 eq 512 cq 384 uq 512 p0 256 p1 256".split()
 for _n, _k in zip(_w[0::2], _w[1::2]):
     SCRATCH[_n + "c"] = ("sbuf", [128, int(_k)], FP8)
     SCRATCH[_n + "s"] = ("sbuf", [128, int(_k)], U8)
@@ -66,18 +57,20 @@ def program(g, core, T, topo):
     acc = {}
     ops = []
     group = {}
+    on_scalar = set(int(k) for k in ON.split())
+    either_n = [0]
 
     def meet(a, b):
         return a[0] < b[1] and b[0] < a[1] and (a[0] - b[0]) % math.gcd(a[2], b[2]) == 0
 
-    def issue(q, fn, reads, writes, sem, n, dur, lat=None):
+    def issue(q, fn, reads, writes, sem, n):
         deps, me = set(), len(ops)
         for w, regs in ((False, reads), (True, writes)):
             for b, lo, hi, st in regs:
                 for a in acc.get(b, []):
-                    if (w or a[3]) and meet((lo, hi, st), a):
+                    if (w or a[3] or (b[:2] == "bk" and ops[a[4]][0] != q)) and meet((lo, hi, st), a):
                         deps.update(group.get(ops[a[4]][3], [a[4]]))
-        ops.append([q, fn, sorted(deps), sem, n, dur, dur if lat is None else lat])
+        ops.append([q, fn, sorted(deps), sem, n])
         if n != 1:
             group.setdefault(sem, []).append(me)
         for w, regs in ((False, reads), (True, writes)):
@@ -134,48 +127,35 @@ def program(g, core, T, topo):
     def val(s):
         return (s[0], s[1]) if isinstance(s, tuple) else (s, [])
 
-    def us(n, c=1.0):
-        return max(64, n * c) * CY
-
     def width(v):
         r0 = v[1][0]
         return -(-(r0[2] - r0[1]) // r0[3])
 
-    def half(*vs):
-        return 0.5 if all(SCRATCH[v[1][0][0]][2] in (BF, U16) for v in vs) else 1.0
-
     def ts(o, i, s1, op0, s2=None, op1=None):
         a, b = val(s1), val(s2)
         rd = i[1] + a[1] + b[1]
-        d = (0.05 + us(width(o), 1.5)) if len(i[1]) > 1 else us(width(o), half(o, i))
         if op1 is None:
-            issue("v", lambda: g.vector.tensor_scalar(o[0], i[0], a[0], None, op0), rd, o[1], "qv", 1, d)
+            issue("v", lambda: g.vector.tensor_scalar(o[0], i[0], a[0], None, op0), rd, o[1], "qv", 1)
         else:
-            issue("v", lambda: g.vector.tensor_scalar(o[0], i[0], a[0], b[0], op0, op1), rd, o[1], "qv", 1, d)
+            issue("v", lambda: g.vector.tensor_scalar(o[0], i[0], a[0], b[0], op0, op1), rd, o[1], "qv", 1)
 
     def tt(o, a, b, op):
-        issue("v", lambda: g.vector.tensor_tensor(o[0], a[0], b[0], op), a[1] + b[1], o[1], "qv", 1,
-              (0.05 + us(width(o), 1.5)) if len(a[1]) > 1 else us(width(o), 1 if a[1][0][0][:2] == "bk" else 2))
+        issue("v", lambda: g.vector.tensor_tensor(o[0], a[0], b[0], op), a[1] + b[1], o[1], "qv", 1)
 
-    def cp(o, i, n=None):
-        n = n or width(o)
-        issue("v", lambda: g.vector.tensor_copy(o[0], i[0]), i[1], o[1], "qv", 1,
-              (0.05 + us(n, 1.5)) if len(i[1]) > 1 else us(n, half(o, i)))
-
-    def fill(o, c):
-        issue("v", lambda: g.vector.memset(o[0], c), [], o[1], "qv", 1, us(width(o), half(o)))
+    def cp(o, i):
+        issue("v", lambda: g.vector.tensor_copy(o[0], i[0]), i[1], o[1], "qv", 1)
 
     def red(o, i):
-        issue("v", lambda: g.vector.tensor_reduce(o[0], i[0], AxisListType.X, OP.add), i[1], o[1], "qv", 1, us(width(i)))
+        issue("v", lambda: g.vector.tensor_reduce(o[0], i[0], AxisListType.X, OP.add), i[1], o[1], "qv", 1)
 
     def scan(o, a, b, op0, op1, init=0.0):
-        issue("v", lambda: g.vector.tensor_tensor_scan(o[0], a[0], b[0], init, op0, op1), a[1] + b[1], o[1], "qv", 1, us(width(o), half(o, a)))
+        issue("v", lambda: g.vector.tensor_tensor_scan(o[0], a[0], b[0], init, op0, op1), a[1] + b[1], o[1], "qv", 1)
 
     def qz(c, s, i):
-        issue("v", lambda: g.vector.quantize_mx(c[0], s[0], i[0]), i[1], c[1] + s[1], "qv", 1, 0.02 + width(i) * 0.26e-3)
+        issue("v", lambda: g.vector.quantize_mx(c[0], s[0], i[0]), i[1], c[1] + s[1], "qv", 1)
 
-    def act(o, i, f=AF.Copy, bias=None, scale=None, accum=None, lock=(), n=None):
-        kw, rd, wr = {}, list(i[1]), list(o[1]) + list(lock)
+    def act(o, i, f=AF.Copy, bias=None, scale=None, accum=None):
+        kw, rd, wr = {}, list(i[1]), list(o[1])
         if bias is not None:
             kw["bias"] = val(bias)[0]
             rd += val(bias)[1]
@@ -185,34 +165,67 @@ def program(g, core, T, topo):
         if accum is not None:
             kw["accum_out"] = accum[0]
             wr += accum[1]
-        n = n or width(o)
-        issue("s", lambda: g.scalar.activation(o[0], i[0], f, **kw), rd, wr, "qs", 1,
-              (0.08 + us(n, 1.5)) if len(i[1]) > 1 else 0.03 + us(n))
+        issue("s", lambda: g.scalar.activation(o[0], i[0], f, **kw), rd, wr, "qs", 1)
+
+    def scalar_turn():
+        either_n[0] += 1
+        return either_n[0] - 1 in on_scalar
+
+    def lin(o, i, scale=None, bias=None):
+        if scalar_turn():
+            act(o, i, AF.Identity if isinstance(bias, tuple) else AF.Copy, bias, scale)
+        elif scale is None and bias is None:
+            cp(o, i)
+        elif bias is None:
+            ts(o, i, scale, OP.mult)
+        elif scale is None:
+            ts(o, i, bias, OP.add)
+        else:
+            ts(o, i, scale, OP.mult, bias, OP.add)
+
+    def fill(o, c, fixed=False):
+        if not fixed and scalar_turn():
+            act(o, R("one", 0, width(o)), AF.Copy, scale=c)
+        else:
+            issue("v", lambda: g.vector.memset(o[0], c), [], o[1], "qv", 1)
+
+    def total(o, x, junk):
+        if scalar_turn():
+            act(junk, x, AF.Identity, accum=o)
+        else:
+            red(o, x)
 
     def mm(o, lc, ls, rc, rs, start=True, stop=True):
         issue("t", lambda: g.tensor.matmul_mx(o[0], lc[0], ls[0], rc[0], rs[0], start, stop),
-              lc[1] + ls[1] + rc[1] + rs[1], o[1], "qt", 1, us(width(rc) + 16, 1.25))
+              lc[1] + ls[1] + rc[1] + rs[1], o[1], "qt", 1)
+
+    def mq(o, l, a, m, b, n=128, start=True, stop=True):
+        mm(R("bk%d" % o, 0, n), R(l + "c", a, a + 128), R(l + "s", a, a + 128), R(m + "c", b, b + n), R(m + "s", b, b + n), start, stop)
+
+    def qq(d, a, n, i):
+        qz(R(d + "c", a, a + n), R(d + "s", a, a + n), i)
 
     def iota(o, pat, base, cm):
-        issue("p", lambda: g.iota(o[0], pat, base, cm, allow_small_or_imprecise_dtypes=True), [], o[1], "qp", 1, 0.13 + us(width(o), 2))
+        issue("p", lambda: g.iota(o[0], pat, base, cm, allow_small_or_imprecise_dtypes=True), [], o[1], "qp", 1)
 
-    def resets(o, a, b):
-        issue("p", lambda: g.affine_select(o[0], T.ones[:, 0:a * b], [[0, a], [1, b]], OP.not_equal, 0.0, 0, 0), R("ones", 0, a * b)[1], o[1], "qp", 1,
-              0.17 + us(a * b, 2))
+    def resets(o, a, b, i=None, c=0.0):
+        i = i or R("ones", 0, a * b)
+        issue("p", lambda: g.affine_select(o[0], i[0], [[0, a], [1, b]], OP.not_equal, c, 0, 0), i[1], o[1], "qp", 1)
 
     def pickout(o, i, base, cm):
-        issue("p", lambda: g.affine_select(o[0], i[0], [[-1, width(o)]], OP.is_equal, 0.0, base, cm), i[1], o[1], "qp", 1, 0.17 + us(width(o), 2))
-
-    def sfill(o, c):
-        act(o, R("one", 0, width(o)), AF.Copy, scale=c)
+        issue("p", lambda: g.affine_select(o[0], i[0], [[-1, width(o)]], OP.is_equal, 0.0, base, cm), i[1], o[1], "qp", 1)
 
     def dma(q, sem, out, i):
-        issue(q, lambda: Q[q].dma_start(out[0], i[0]), i[1], out[1], sem, 16, 0.07, 2.5)
+        issue(q, lambda: Q[q].dma_start(out[0], i[0]), i[1], out[1], sem, 16)
+
+    def bank(k, n, a=0):
+        return R("bk%d" % k, a, a + n)
 
     for gr in range(8):
         dma("ys"[gr % 2], "lnb", (T.nbw[16 * gr:16 * gr + 16, :], [("nbw", 0, 48, 1)] if gr == 0 else []), (T.nb[:, :], []))
-    dma("s", "lx", R("xt"), (T.x[:, :], []))
-    dma("s", "lx2", R("P1", 72, 520), (T.x[:, 0:448], []))
+    dma("y", "lx", R("xt"), (T.x[:, :], []))
+    dma("y", "lx2", R("P1", 72, 512), (T.x[:, 0:440], []))
+    dma("y", "lx3", R("UC", 64, 512), (T.x[:, 0:448], []))
     first = True
     for k in range(3):
         i = 0
@@ -224,80 +237,63 @@ def program(g, core, T, topo):
             i, first = i + n, False
     for gr in range(8):
         dma("y", "lnn", (T.nn[16 * gr:16 * gr + 16, :], [("nn", 0, 138, 1)] if gr == 0 else []), (T.nst[:, :], [("nst", 0, 138, 1)]))
-    for b, lo, hi in (("P2", 256, 640), ("U0", 128, 576), ("U1", 320, 576)):
-        dma("y", "lx3", R(b, lo, hi), (T.x[:, 0:hi - lo], []))
     dma("y", "lw", R("wt"), (T.w[:, :], []))
     nl = [R("nn", 46 * k, 46 * k + 46, 3) for k in range(3)]
 
-    iota(R("pp", 0, 1), [[0, 1]], 0, 1)
-    iota(R("pp", 1, 2), [[0, 1]], 10, 11)
-    iota(R("k3"), [[0, 16], [1, 3]], 0, 0)
+    iota(R("pp", 0, 2), [[128, 2]], 0, 1)
+    iota(R("pp", 2, 3), [[0, 1]], 10, 11)
+    iota(R("k3"), [[0, 16], [16, 3]], 0, 0)
     iota(R("t48"), [[16, 16], [0, 3]], 256 * r, 0)
-    iota(R("g24"), [[0, 2], [1, 8], [0, 3]], 0, 0)
-    iota(R("rowd"), [[0, 8], [2, 16]], 0, 0)
-    iota(R("g48"), [[0, 6], [1, 8]], 0, 0)
-    iota(R("rowb"), [[0, 16], [1, 16]], 0, 0)
-    iota(R("j64"), [[0, 4], [1, 16]], 0, 0)
-    iota(R("d8"), [[0, 2], [1, 4]], 0, 0)
+    iota(R("g24"), [[0, 2], [16, 8], [0, 3]], 0, 0)
     iota(R("tab", 1792, 2304), [[1, 512]], 1792, 0)
-    fill(R("one", 0, 256), 1.0)
+    iota(R("rowd"), [[0, 8], [2, 16]], 0, 0)
+    iota(R("rowb"), [[0, 8], [1, 16]], 0, 0)
+    iota(R("j64"), [[0, 4], [1, 16]], 0, 0)
+    iota(R("d8"), [[0, 2], [32, 4]], 0, 0)
+    iota(R("qn"), [[-16, 16], [-4, 2], [-1, 2]], -3, 0)
+    iota(R("c44", 0, 2), [[1, 2]], 10, 0)
+    iota(R("s4"), [[-128, 2], [0, 2]], 256, -1)
+    fill(R("one", 0, 256), 1.0, True)
     scan(R("iob"), R("one", 0, 256), R("one", 0, 256), OP.add, OP.mult, -1.0)
-    fill(R("one", 256, 516), 1.0)
-    act(R("ones"), R("one", 0, 128))
+    fill(R("one", 256, 516), 1.0, True)
+    lin(R("ones"), R("one", 0, 128))
 
-    def c(k):
-        return R("ci", k, k + 1)
+    def c(k, n=1):
+        return R("ci", k, k + n)
 
     def col(k):
         return R("col", k, k + 1)
-
-    def col2(k):
-        return R("col2", k, k + 1)
-    ts(c(3), R("pp", 1, 2), 15, OP.bitwise_and)
-    ts(c(4), c(3), 3, OP.mult, 2, OP.add)
-    ts(c(5), c(4), 4, OP.arith_shift_right)
-    ts(c(0), R("pp", 0, 1), 15, OP.bitwise_and)
-    ts(c(1), R("pp", 0, 1), 4, OP.arith_shift_right)
-    ts(c(2), R("pp", 0, 1), 5, OP.arith_shift_right)
-    cp(R("col", 0, 6), R("ci"))
-    ts(R("mk48"), R("k3"), col(5), OP.is_equal)
-    ts(R("gmt"), R("g24"), col(1), OP.is_equal)
+    p0, p01 = R("pp", 0, 1), R("pp", 0, 2)
+    ts(c(3), R("pp", 2, 3), 15, OP.bitwise_and)
+    ts(col(9), c(3), 3.0, OP.mult, 2.0, OP.add)
+    ts(c(0), p0, 15, OP.bitwise_and)
+    ts(c(6, 2), p01, 240, OP.bitwise_and)
+    cp(col(3), c(3))
+    cp(R("col", 6, 8), R("ci", 6, 8))
+    ts(c(1), p0, 1, OP.bitwise_and)
+    ts(c(2), p0, 96, OP.bitwise_and)
+    ts(c(8), p0, 15, OP.bitwise_and, 2, OP.arith_shift_right)
+    cp(col(0), c(0))
+    cp(R("col", 1, 3), R("ci", 1, 3))
+    cp(col(8), c(8))
+    lin(col(11), col(0), 2.0)
+    ts(R("mk48"), R("k3"), col(0), OP.add, col(9), OP.is_equal)
+    ts(R("gmt"), R("g24"), col(6), OP.is_equal)
+    gm = R("gmt", 0, 48, 3)
     ts(R("rs3"), R("k3"), 0.0, OP.not_equal)
     fill(R("rs24"), 1.0)
     fill(R("rs24", 0, 48, 24), 0.0)
-    act(R("gl48"), R("t48"), AF.Identity, bias=col(3))
-    act(R("own48"), R("gl48"), AF.Copy, bias=256.0 * (1 - r))
+    lin(R("gl48"), R("t48"), None, col(3))
+    lin(R("own48"), R("gl48"), None, 256.0 * (1 - r))
     for b in range(7):
-        if b % 2:
-            act(R("tab", 256 * b, 256 * b + 256), R("iob"), AF.Copy, bias=256.0 * b)
-        else:
-            ts(R("tab", 256 * b, 256 * b + 256), R("iob"), 256.0 * b, OP.add)
-    act(R("rowc"), R("rowd"), AF.Copy, bias=-255.0)
-    act(R("tkc", 0, 16), R("iob", 0, 16), AF.Copy, bias=RND - 64.0 * r, scale=32.0)
+        lin(R("tab", 256 * b, 256 * b + 256), R("iob"), None, 256.0 * b)
+    lin(R("rowc"), R("rowd"), None, -255.0)
+    lin(R("tkc", 0, 16), R("iob", 0, 16), 32.0, RND - 64.0 * r)
     ts(R("tkw"), R("iob", 0, 16), 2.0 * r, OP.is_lt, 512.0, OP.mult)
     tt(R("tkc", 0, 16), R("tkc", 0, 16), R("tkw"), OP.add)
     for k in range(2):
-        act(R("tkc", 16 + k, 17 + k), R("iob", 2 * r + 1 - k, 2 * r + 2 - k), AF.Copy, bias=RND, scale=32.0)
-    for h in range(2):
-        act(R("nv", 2 * h, 2 * h + 1), col(1), AF.Copy, bias=128.0 * h, scale=16.0)
-        act(R("nv", 2 * h + 1, 2 * h + 2), col(3), AF.Copy)
-    ts(R("gm"), R("g48"), col(1), OP.is_equal)
-    resets(R("rs8"), 6, 8)
-    resets(R("rs16"), 4, 16)
-    ts(R("dm"), R("j64"), col(0), OP.is_equal)
-    act(R("jl"), R("iob", 0, 16), AF.Identity, bias=col(0), scale=16.0)
-    act(R("jw"), R("jl"), AF.Copy, bias=256.0)
-    act(R("z", 2, 48, 3), R("jl"))
-    act(col2(0), col(1), AF.Copy, bias=8.0)
-    act(col2(1), col(0), AF.Copy, scale=2.0)
-    act(col2(2), col(0), AF.Copy, bias=1.0, scale=2.0)
-    sfill(R("P1", 520, 584), 0.0)
-    for h in range(2):
-        act(R("P1", 522 + 30 * h, 552 + 32 * h, 4), R("gm", 0, 8), AF.Copy, scale=64.0 * r)
-    act(R("sqa"), R("rowb", 0, 128), AF.Square, bias=col(3), scale=-1.0)
-    for e in range(4):
-        act(R("pa", 512 + e, 1024, 4), R("sqa"), AF.Relu, bias=1.0, scale=-1.0)
-    qz(R("pac", 128, 256), R("pas", 128, 256), R("pa", 512, 1024))
+        lin(R("tkc", 16 + k, 17 + k), R("iob", 2 * r + 1 - k, 2 * r + 2 - k), 32.0, RND)
+    nv = [col(6), col(3), col(7), col(3)]
 
     tt(R("n2m"), R("nbw"), R("mk48"), OP.mult)
     ts(R("hi"), R("nbw"), 1792, OP.bitwise_and)
@@ -309,7 +305,7 @@ def program(g, core, T, topo):
     scan(R("ks"), R("rs3"), R("kf"), OP.mult, OP.add)
     scan(R("kc"), R("rs24"), R("km"), OP.mult, OP.add)
     cp(R("ku"), R("ks", 2, 48, 3))
-    act(R("jk"), ind(R("tab"), R("ku")), AF.Sign, bias=R("kc", 23, 24), scale=-1.0, accum=R("ss", 0, 1))
+    act(R("jk", 0, 256), ind(R("tab"), R("ku")), AF.Sign, bias=R("kc", 23, 24), scale=-1.0, accum=R("ss", 0, 1))
     ts(R("kr"), ind(R("tab"), R("ku")), R("kc", 47, 48), OP.is_lt, 2.0, OP.mult)
     scan(R("krs"), R("kr"), R("kr"), OP.add, OP.max)
     p2 = [R("ss", 0, 1), R("krs", 255, 256)]
@@ -319,38 +315,42 @@ def program(g, core, T, topo):
         ts(R("ph", h, h + 1), p2[h], -15.0 if h else 240.0, OP.add, RND, OP.add)
         ts(hi2[h], R("ph", h, h + 1), -RND, OP.add)
     for e in range(4):
-        ts(R("P1", e, 72, 4), R("tkc"), R("ph", e // 2, e // 2 + 1), OP.is_equal, R("nv", e, e + 1), OP.mult)
-    qz(R("pmc", 0, 128), R("pms", 0, 128), R("P1", 0, 512))
+        ts(R("P1", e, 72, 4), R("tkc"), R("ph", e // 2, e // 2 + 1), OP.is_equal, nv[e], OP.mult)
+    qq("pm", 0, 128, R("P1", 0, 512))
     for e in range(4):
         ts(R("pa", e, 512, 4), rw[e // 2], hi2[e // 2], OP.add, p2[e // 2], OP.is_equal)
-    qz(R("pac", 0, 128), R("pas", 0, 128), R("pa", 0, 512))
-    mm(R("bk6", 0, 128), R("pac", 0, 128), R("pas", 0, 128), R("pmc", 0, 128), R("pms", 0, 128))
-    cp(R("l18"), R("bk6", 0, 18))
+    qq("pa", 0, 128, R("pa", 0, 512))
+    mq(6, "pa", 0, "pm", 0)
+    cp(R("l18"), bank(6, 18))
+    qq("q0", 0, 256, R("xt"))
+    act(R("sqa"), R("rowb"), AF.Square, bias=col(3), scale=-1.0)
+    for e in range(4):
+        act(R("pa", 512 + e, 1024, 4), R("sqa"), AF.Relu, bias=1.0, scale=-1.0)
+    qq("pa", 128, 128, R("pa", 512, 1024))
     ts(R("lo", 0, 1), p2[0], 255.0, OP.add, hi2[0], OP.subtract)
     ts(R("lo", 1, 2), p2[1], hi2[1], OP.subtract)
+    lin(R("P1", 514, 576, 4), gm, 64.0 * r)
     for h in range(2):
+        a, g8 = 512 + 32 * h, R("gmt", 0, 24, 3)
         ts(R("wr", h, h + 1), p2[h], 257.0 + 255 * h - 64 * r, OP.is_ge, -512.0, OP.mult)
-    for h in range(2):
-        a = 520 + 34 * h
         if h == 0:
-            act(R("P1", a, 552, 4), R("gm", 0, 8), AF.Copy, scale=hi2[0])
+            lin(R("P1", a, a + 32, 4), g8, hi2[0])
         else:
-            ts(R("P1", a, 584, 4), R("gm", 0, 8), hi2[1], OP.mult)
-        act(R("P1", a + 1, 552 + 32 * h, 4), R("gm", 0, 8), AF.Copy, scale=R("lo", h, h + 1))
-        act(R("P1", 523 + 30 * h, 552 + 32 * h, 4), R("gm", 0, 8), AF.Copy, scale=R("wr", h, h + 1))
-    qz(R("pmc", 128, 256), R("pms", 128, 256), R("P1", 72, 584))
-    mm(R("bk5", 0, 128), R("pac", 128, 256), R("pas", 128, 256), R("pmc", 128, 256), R("pms", 128, 256))
-    ts(R("pl"), R("bk5", 112, 128), 0.5, OP.mult)
-    act(R("z", 98, 144, 3), R("bk5", 112, 128), AF.Copy, scale=0.5, lock=R("bk5")[1])
+            ts(R("P1", a, a + 32, 4), g8, hi2[1], OP.mult)
+        lin(R("P1", a + 1, a + 32, 4), g8, R("lo", h, h + 1))
+        lin(R("P1", a + 3, a + 32, 4), g8, R("wr", h, h + 1))
+    qq("pm", 128, 128, R("P1", 64, 576))
+    mq(7, "pa", 128, "pm", 128)
+    ts(R("pl"), bank(7, 16, 112), 0.5, OP.mult)
+    lin(R("plf"), bank(7, 16, 112), 0.5)
     act(R("posn"), ind(R("iob"), R("pl")))
-    qz(R("q0c"), R("q0s"), R("xt"))
 
-    def pick(dc, ds, a, b, sc, ss, w0, w1, off, own=False):
-        oc, os = R(dc, a, b), R(ds, a, b)
+    def pick(d, a, b, s, w0, w1, off, own=False):
+        oc, os = R(d + "c", a, b), R(d + "s", a, b)
         if own:
-            oc, os = (oc[0], [(dc, 0, 256, 1)]), (os[0], [(ds, 0, 256, 1)])
-        cp(W32(oc), ind(W32(R(sc, w0, w1)), off), b - a)
-        act(os, ind(R(ss, w0, w1), off), n=b - a)
+            oc, os = (oc[0], [(d + "c", 0, 256, 1)]), (os[0], [(d + "s", 0, 256, 1)])
+        cp(W32(oc), ind(W32(R(s + "c", w0, w1)), off))
+        act(os, ind(R(s + "s", w0, w1), off))
 
     others = [d for d in range(1, 8)]
     far = [d for d in others if topo.die(T.cores[r ^ d]) != topo.die(core)]
@@ -370,278 +370,209 @@ def program(g, core, T, topo):
                                             remote_sem=T.sem[sem], src=srcs(blk[r ^ d]), dst=dsts(blk[r ^ d])))
             g.remote_dma_fused(tf, local_sem=T.sem.loc)
             cnt["loc"] = cnt.get("loc", 0) + 14
-        me = issue("p", call, [(b, lo, hi, 1) for b, lo, hi in regs], [], None, 1, 0.7, 0.7)
+        me = issue("p", call, [(b, lo, hi, 1) for b, lo, hi in regs], [], None, 1)
         group.setdefault(sem, []).append(len(ops))
-        ops.append(["a", None, [me], sem, 14, 0.0, 2.5])
+        ops.append(["a", None, [me], sem, 14])
 
     def arrive(sem, b, lo, hi):
         acc.setdefault(b, []).append((lo, hi, 1, True, group[sem][0]))
 
-    def send_w(bc, bs, sem):
+    def send_w(b, sem):
+        bc, bs = b + "c", b + "s"
         send(lambda q: T[bc][:, 256 + 32 * q:288 + 32 * q].bitcast(dt.uint8), lambda q: T[bc][:, 32 * q:32 * q + 32].bitcast(dt.uint8),
              sem, [(bc, 256, 512)])
         send(lambda q: T[bs][:, 256 + 32 * q:288 + 32 * q], lambda q: T[bs][:, 32 * q:32 * q + 32], sem, [(bs, 256, 512)])
-
-    def bank(k, n, a=0):
-        return R("bk%d" % k, a, a + n)
-
-    def gram(bc, bs, mc, ms, m0):
-        mm(bank(0, 256), R(bc, 256, 384), R(bs, 256, 384), R(mc, m0, m0 + 256), R(ms, m0, m0 + 256))
-        for k, j in enumerate((1, 3)):
-            a = m0 + 128 * k
-            mm(bank(j, 128), R(bc, 384, 512), R(bs, 384, 512), R(mc, a, a + 128), R(ms, a, a + 128))
-        act(R("gs", 0, 256), bank(0, 256))
-        cp(R("gs", 264, 392), bank(1, 128))
-        cp(R("gs", 392, 520), bank(3, 128))
-
-    BK = [[0, 4, 5, 6], [0, 1, 2, 3]]
-
-    def dec(h, b, cc, cs, a, start):
-        w = 256 if b == 0 else 128
-        mm(bank(BK[h][b], w), R("eqc", 128 * b, 128 * b + 128), R("eqs", 128 * b, 128 * b + 128),
-           R(cc, a + 128 * h, a + 128 * h + w), R(cs, a + 128 * h, a + 128 * h + w), start, not start)
 
     def diagonal(o, x, i, off):
         tt(x, ind(i, off), R("dm"), OP.mult)
         scan(o, R("rs16"), x, OP.mult, OP.add)
 
-    def local_scores(t):
+    def decode(k0, s, a, start):
+        for h, b in k0:
+            mq(b + 3 * h, "eq", 128 * b, s, a + 128 * h, 128 if b else 256, start, not start)
+
+    def local_scores(t, b, m, m0):
         for h in range(2):
-            tt(R("gg", 32 * h, 32 * h + 32), ind(R("gs", 264 * h, 264 * h + 264), R("xoa" if t else "xo", 2 * h, 2 * h + 2)), R("dm", 0, 32), OP.mult)
-        scan(R("sc"), R("rs16"), R("gg"), OP.mult, OP.add)
-        s0, s1 = R("sc", 15, 64, 32), R("sc", 31, 64, 32)
-        m, ma, mx = "m%d" % t, "ma%d" % t, "mx%d" % t
+            mq(4 + h, b, 256 + 128 * h, m, m0, 256)
+            lin(R("gs", 256 * h, 256 * h + 256), bank(4 + h, 256))
         for h in range(2):
-            ts(R(ma, 4 * h, 4 * h + 4), R("msk", 4 * h, 4 * h + 4), R("sc", 15 + 32 * h, 16 + 32 * h), OP.max, R("sc", 31 + 32 * h, 32 + 32 * h), OP.max)
+            tt(R("gg", 34 * h + 1, 34 * h + 33), ind(R("gs", 256 * h, 256 * h + 256), R("xp" if t else "xo", 2 * h, 2 * h + 2)), R("dm", 0, 32), OP.mult)
+        scan(R("sc"), R("rs17"), R("gg"), OP.mult, OP.add)
+        s1, s0 = R("sc", 16, 68, 34), R("sc", 33, 68, 34)
+        ma, mx = "ma%d" % t, "mx%d" % t
+        tt(R("m%d" % t), s0, s1, OP.max)
+        for h in range(2):
+            ts(R(ma, 4 * h, 4 * h + 4), R("msk", 4 * h, 4 * h + 4), R("sc", 16 + 34 * h, 17 + 34 * h), OP.add, R("sc", 33 + 34 * h, 34 + 34 * h), OP.max)
         send(lambda q: T[ma][:, q:q + 1], lambda q: T[mx][:, q:q + 1], "e%d" % t, [(ma, 0, 8)])
-        b = 32 * (lb % 4)
-        rest = [(0, b), (b + 32, 128)] if 0 < b < 96 else [(32 - b // 3, 64), (64, 128 - b // 3)]
-        for i, (lo, hi, to) in enumerate([(b, b + 16, b + 16), (b + 16, b + 32, b)] + [(lo, hi, lo) for lo, hi in rest]):
+        o = 32 * (lb % 4)
+        rest = [(0, o), (o + 32, 128)] if 0 < o < 96 else [(32 - o // 3, 64), (64, 128 - o // 3)]
+        for i, (lo, hi, to) in enumerate([(o, o + 16, o + 16), (o + 16, o + 32, o)] + [(lo, hi, lo) for lo, hi in rest]):
             dma("y", "lm%d" % t, (T[mx][to:to + hi - lo, lb:lb + 1], [(mx, 0, 8, 1)] if i == 0 else []), (T[ma][lo:hi, lb:lb + 1], [(ma, 0, 8, 1)]))
-        tt(R(m), s0, s1, OP.max)
         tt(R("sm", 0, 2), s0, s1, OP.is_ge)
-        act(R("sm", 2, 6, 2), R("sm", 0, 2), AF.Copy, bias=-4e29, scale=4e29)
-        act(R("sm", 3, 6, 2), R("sm", 0, 2), AF.Copy, scale=-4e29)
-        tt(R("sm", 8, 12), R("sc", 15, 64, 16), R("sm", 2, 6), OP.add)
 
-    def statics(t, hi_own, hl):
+    def ahead(t, b):
+        sel, ct, ns = "sel%d" % t, "ct%d" % t, "ns%d" % t
         for h in range(2):
-            a = 128 * t + 64 * h
-            act(R("mn", a, a + 64, 2), R("j64", 0, 32), AF.Square, bias=hi_own[h], scale=-1.0)
-            for k in range(2):
-                act(R("mn", a + 32 * k + 1, a + 32 * k + 32, 2), R("j64", 0, 16), AF.Square, bias=R("hl", hl + 2 * h + k, hl + 2 * h + k + 1), scale=-1.0)
-            act(R("nat", 32 * t + 16 * h, 32 * t + 16 * h + 16), R("mn", a, a + 32, 2), AF.Relu, bias=0.0625, scale=-0.0625)
+            lin(R("st", h, 16, 2), R("dif", h, 16, 2), R("sm", h, h + 1))
+        tt(R(sel), R("st"), R("hl", 0, 32, 2), OP.add)
+        tt(R("gd"), ind(R(sel), R("cof")), R("gm2"), OP.mult)
+        s = 2 * (1 - t)
         for h in range(2):
-            for k in range(2):
-                a = 64 * h + 32 * k
-                act(R("mq", a, a + 32), R("mn", 128 * t + a, 128 * t + a + 32), AF.Identity,
-                    bias=R("sm", 8 + 2 * h + k, 9 + 2 * h + k), scale=-8e29)
+            ts(R(ct, 2 + h, 512, 4), R("rowb"), R(sel, 4 + s + h, 5 + s + h), OP.is_equal, BIG, OP.mult)
+            lin(R(ns, 128 * h + 1, 128 * h + 128, 2), R("qm"), None, R(sel, s + h, s + h + 1))
+        qq("cq", 128 * t, 128, R(ct))
+        decode(((0, 0), (0, 1), (0, 2), (0, 3)), b, 256, True)
 
-    def weights(t, lo_own, hl):
-        if t == 0:
-            act(R("sqb"), R("rowb"), AF.Square, bias=col(0), scale=-1.0)
+    def choose(t, b, u):
+        mx, m, p = "mx%d" % t, "m%d" % t, "p%d" % t
+        arrive("a%d" % t, b + "c", 0, 256)
+        arrive("a%d" % t, b + "s", 0, 256)
         for h in range(2):
-            if t == 0:
-                act(R("ct", h, 1024, 4), R("sqb"), AF.Relu, bias=BIG, scale=-BIG)
-            else:
-                ts(R("ct", 1024 * t + h, 1024 * t + 1024, 4), R("rowb"), lo_own[h], OP.is_equal, BIG, OP.mult)
-            for k in range(2):
-                a = 1024 * t + 512 * k
-                ts(R("ct", a + 2 + h, a + 512, 4), R("rowb", 0, 128), R("hl", hl + 2 * h + k, hl + 1 + 2 * h + k), OP.is_equal, BIG, OP.mult)
-        qz(R("cqc", 256 * t, 256 * t + 256), R("cqs", 256 * t, 256 * t + 256), R("ct", 1024 * t, 1024 * t + 1024))
-
-    def flags_times(t, k, b, qc, qs, uq):
-        ca = 256 * t + 128 * k
-        mm(bank(b, 128), R("cqc", ca, ca + 128), R("cqs", ca, ca + 128), R(qc, uq, uq + 128), R(qs, uq, uq + 128))
-
-    def choose(t, bc, bs):
-        u, uq, z, xl = "U%d" % t, 128 * t, 96 * t, "xl%d" % t
-        arrive("a%d" % t, bc, 0, 256)
-        arrive("a%d" % t, bs, 0, 256)
+            mq(4 + h, b, 256 + 128 * h, b, 128 * h)
+            tt(R("xd", 129 * h, 129 * h + 128), bank(4 + h, 128), R("idn"), OP.mult)
+            total(R("sm", 16 + h, 17 + h), R("xd", 129 * h, 129 * h + 128 + t), R("jk", 130 * h, 130 * h + 128 + t))
+            ts(R("sm", 18 + h, 19 + h), R(m, h, h + 1), R("sm", 16 + h, 17 + h), OP.is_ge, R("sel%d" % t, 8 + h, 9 + h), OP.mult)
+            ts(R("UC", 32 * h, 32 * h + 32, 2), R("gd", 16 * h, 16 * h + 16), R("sm", 18 + h, 19 + h), OP.mult, R("sel%d" % t, 14 + h, 15 + h), OP.mult)
+        qq("uq", 128 * t, 128, R("UC"))
+        mq(6, "cq", 256, "uq", 128 * t)
+        ts(R("lp", 16 * t, 16 * t + 16), bank(6, 16), 1.0 / BIG, OP.mult)
+        decode(((1, 1), (1, 2), (1, 3)), b, 256, True)
         for h in range(2):
-            mm(bank(2 + h, 128), R(bc, 256 + 128 * h, 384 + 128 * h), R(bs, 256 + 128 * h, 384 + 128 * h),
-               R(bc, 128 * h, 128 * h + 128), R(bs, 128 * h, 128 * h + 128))
+            pick(p, 128 * h, 128 * h + 128, b, 0, 512, R("lp", 16 * t + 8 * h, 16 * t + 8 * h + 8))
+        decode(((0, 1), (0, 2), (0, 0), (0, 3), (1, 1), (1, 2), (1, 3)), p, 0, False)
         for h in range(2):
-            tt(R("xd", 129 * h, 129 * h + 128), bank(2 + h, 128), R("idn"), OP.mult)
-        act(R("jk", 0, 128 + t), R("xd", 0, 128 + t), AF.Identity, accum=R("sm", 16, 17))
-        red(R("sm", 17, 18), R("xd", 129, 257 + t))
-        for h in range(2):
-            ts(R(u, h, 128, 2), R("mq", 64 * h, 64 * h + 64), R("sm", 16 + h, 17 + h), OP.is_ge)
-        qz(R("uqc", uq, uq + 128), R("uqs", uq, uq + 128), R(u, 0, 512))
-        for k in range(2):
-            flags_times(t, k, 2 + k, "uqc", "uqs", uq)
-        for k in range(2):
-            tt(R("z", z + k, z + 48, 3), bank(2 + k, 16, 16 * k), R(xl, 16 * k, 16 * k + 16), OP.add)
-        scan(R("z", z + 48, z + 96), R("rs3"), R("z", z, z + 48), OP.mult, OP.max)
-        cp(R("lp", 16 * t, 16 * t + 16), R("z", z + 50, z + 96, 3))
-
-    def decide(t):
-        mx, u = "mx%d" % t, "U%d" % t
+            for e in range(4):
+                lin(R("nt", 512 * h + e, 512 * h + 512, 4), bank(e + 3 * h, 128) if e else bank(0, 128, 128 * h), 0.5)
+            qq(b, 512 + 128 * h, 128, R("nt", 512 * h, 512 * h + 512))
         arrive("e%d" % t, mx, 0, 8)
         for h in range(2):
-            ts(R("ofx", 4 * h, 4 * h + 4), R(mx, 4 * h, 4 * h + 4), R("sm", 16 + h, 17 + h), OP.is_lt, col2(1), OP.add)
-        for h in range(2):
-            act(R("jq", 64 * h, 64 * h + 64), ind(R("dw"), R("ofx", 4 * h, 4 * h + 4)), AF.Copy, accum=R("sm", 20 + h, 21 + h))
-        tt(R("sm", 22, 24), R("sm", 16, 18), R("m%d" % t), OP.is_gt)
-        for h in range(2):
-            ts(R(u, 576 + h, 640, 4), R("nat", 32 * t + 16 * h, 32 * t + 16 * h + 16), R("sm", 20 + h, 21 + h), OP.mult, R("sm", 22 + h, 23 + h), OP.mult)
-        vq = 256 + 128 * t
-        qz(R("uqc", vq, vq + 128), R("uqs", vq, vq + 128), R(u, 128, 640))
-        flags_times(t, 0, 7, "uqc", "uqs", vq)
-        a = 48 * t
-        ts(R("lnf", a, a + 16), R("z", 96 * t + 50, 96 * t + 96, 3), 256.0, OP.is_ge, 256.0, OP.mult)
-        tt(R("lnf", a + 16, a + 32), R("lnf", a, a + 16), R("jl" if t else "jw"), OP.add)
-        tt(R("lnf", a + 32, a + 48), bank(7, 16, 112), R("lnf", a + 16, a + 32), OP.add)
-        cp(R("ln", 20 * t, 20 * t + 16), R("lnf", a + 32, a + 48))
+            ts(R("ofx", 4 * h, 4 * h + 4), R(mx, 4 * h, 4 * h + 4), R("sm", 16 + h, 17 + h), OP.is_ge, col(11), OP.add)
+            act(R("jq", 64 * h, 64 * h + 64), ind(R("dw"), R("ofx", 4 * h, 4 * h + 4)), AF.Relu, bias=R("sm", 18 + h, 19 + h),
+                accum=R("sm", 20 + h, 21 + h))
+            ts(u(h), R("ns%d" % t, 128 * h, 128 * h + 128), R("sm", 20 + h, 21 + h), OP.add, R("sm", 18 + h, 19 + h), OP.is_equal)
 
-    def own_parts(cc, cs, a):
-        for h, b in ((0, 0), (0, 1), (0, 2), (0, 3), (1, 1)):
-            dec(h, b, cc, cs, a, True)
+    def final_list(t, a):
+        tt(R("z"), bank(7, 64, a), R("plx%d" % t), OP.add)
+        scan(R("zs"), R("rs4", 0, 64), R("z"), OP.min, OP.max)
+        cp(R("ln", 20 * t, 20 * t + 16), R("zs", 3, 64, 4))
 
-    def merge(t, bc, bs, cc, cs, own, base):
-        pc, psn, off = "p%dc" % t, "p%ds" % t, 16 * t
-        for h in range(2):
-            pick(pc, psn, 128 * h, 128 * h + 128, bc, bs, 0, 512, R("lp", off + 8 * h, off + 8 * h + 8))
-        for b in range(2, 4):
-            dec(1, b, cc, cs, own, True)
-        for h, b in ((0, 1), (0, 2), (0, 3), (0, 0), (1, 1), (1, 2), (1, 3)):
-            dec(h, b, pc, psn, 0, False)
-        for h in range(2):
-            for b in range(4):
-                oo = R("nt", 512 * h + b, 512 * h + 512, 4)
-                if b == 0:
-                    ts(oo, R("bk0", 128 * h, 128 * h + 128), 0.5, OP.mult)
-                elif b == 2:
-                    ts(oo, bank(BK[h][b], 128), 0.5, OP.mult)
-                else:
-                    act(oo, bank(BK[h][b], 128), AF.Copy, scale=0.5)
-            qz(R(cc, base + 128 * h, base + 128 * h + 128), R(cs, base + 128 * h, base + 128 * h + 128), R("nt", 512 * h, 512 * h + 512))
-
-    def own_block(bc, bs, sc, ss, w, off):
-        pick(bc, bs, 32 * lb, 32 * lb + 32, sc, ss, 0, w, off, True)
-
-    pick("b0c", "b0s", 256, 512, "q0c", "q0s", 0, 256, R("l18", 0, 16))
-    send_w("b0c", "b0s", "a0")
-    own_block("b0c", "b0s", "q0c", "q0s", 256, R("l18", 16, 18))
-    gram("b0c", "b0s", "q0c", "q0s", 0)
-    for k in range(2):
-        ts(R("o01", 16 * k, 16 * k + 16), nl[k], -256.0 * r, OP.add)
+    pick("b0", 256, 512, "q0", 0, 256, R("l18", 0, 16))
+    send_w("b0", "a0")
+    pick("b0", 32 * lb, 32 * lb + 32, "q0", 0, 256, R("l18", 16, 18), True)
+    resets(R("rs8"), 2, 8)
+    resets(R("rs16"), 4, 16)
+    resets(R("rs17"), 4, 17)
+    ts(R("dm"), R("j64"), col(0), OP.is_equal)
+    for a in range(2):
+        ts(R("o01", 16 * a, 16 * a + 16), nl[1 - a], -256.0 * r, OP.add)
     act(R("nr"), ind(R("iob"), R("o01")))
-    tt(R("iv", 0, 16), R("bk6", 0, 16), R("gm", 0, 16), OP.mult)
-    scan(R("iv", 16, 32), R("rs8", 0, 16), R("iv", 0, 16), OP.mult, OP.add)
+    tt(R("iv", 0, 16), bank(6, 16), gm, OP.mult)
+    scan(R("iv", 16, 32), R("rs8"), R("iv", 0, 16), OP.mult, OP.add)
     inv = R("iv", 23, 32, 8)
     cp(R("of4", 0, 4, 2), inv)
     ts(R("of4", 1, 4, 2), inv, 256.0, OP.add)
     diagonal(R("xi", 0, 64), R("xg"), R("nr"), R("of4"))
     cp(R("xo"), R("xi", 15, 64, 16))
+    ts(R("msk"), R("d8"), col(2), OP.not_equal, 2e29, OP.mult)
     for h in range(2):
-        sfill(R("gs", 256 + 264 * h, 264 + 264 * h), -1e29)
-    ts(R("msk", 8, 16), R("d8"), col(2), OP.not_equal, 2e29, OP.mult)
-    ts(R("msk", 0, 8), R("msk", 8, 16), -1e29, OP.add)
-    local_scores(0)
+        fill(R("gg", 34 * h, 34 * h + 34, 33), 0.0)
+    local_scores(0, "b0", "q0", 0)
+    cp(R("xi", 128, 130), inv)
+    ts(R("xi", 130, 132), R("xi", 128, 130), 240, OP.bitwise_and)
+    ts(R("xi", 132, 134), R("xi", 128, 130), 15, OP.bitwise_and)
+    cp(R("hv"), R("xi", 130, 134))
+    for h in range(2):
+        lin(R("ns1", 128 * h, 128 * h + 128, 2), R("qn"), None, R("hv", h, h + 1))
+        ts(R("ct1", h, 512, 4), R("rowb"), R("hv", 2 + h, 3 + h), OP.is_equal, BIG, OP.mult)
     diagonal(R("xi", 64, 128), R("xg2"), R("posn"), R("xo"))
-    cp(R("xi", 143, 160, 16), inv)
-    ts(R("xi", 160, 170), R("xi", 15, 160, 16), 4, OP.arith_shift_right)
-    ts(R("xi", 170, 180), R("xi", 15, 160, 16), 15, OP.bitwise_and)
-    cp(R("hl"), R("xi", 160, 180))
-    statics(0, [col(1), col2(0)], 4)
+    cp(R("xp"), R("xi", 79, 128, 16))
+    ts(R("xi", 136, 144), R("xi", 15, 128, 16), 240, OP.bitwise_and)
+    ts(R("xi", 144, 152), R("xi", 15, 128, 16), 15, OP.bitwise_and)
+    cp(R("hl", 0, 16), R("xi", 136, 152))
+    fill(R("hl", 16, 20, 2), -4.0)
+    fill(R("hl", 17, 20, 2), -8.0)
+    fill(R("hl", 28, 32, 2), -0.25)
+    fill(R("hl", 29, 32, 2), -0.125)
+    tt(R("dl", 0, 4), R("xi", 79, 128, 16), R("s4"), OP.add)
+    ts(R("hl", 20, 24), R("dl"), RND, OP.add, -RND, OP.add)
+    tt(R("hl", 24, 28), R("dl"), R("hl", 20, 24), OP.subtract)
+    tt(R("dif"), R("hl", 1, 32, 2), R("hl", 0, 32, 2), OP.subtract)
     pickout(R("idn"), R("ones"), 0, 1)
-    ts(R("dw"), R("iob", 0, 32), col2(2), OP.is_equal)
-    weights(0, [col(0), col(0)], 14)
-    fill(R("P2", 0, 256), 0.0)
-    act(R("gms"), R("gm", 0, 8), AF.Copy, scale=1.0 / BIG)
-    for k in range(2):
-        for h in range(2):
-            a = 64 * k + 33 * h
-            ts(R("P2", a, 64 * k + 32 * h + 32, 4), R("gm", 0, 8), R("hl", 4 + 2 * h + k, 5 + 2 * h + k), OP.mult, 16.0 / BIG, OP.mult)
-            act(R("P2", a + 128, 64 * k + 32 * h + 160, 4), R("gms"), AF.Copy, scale=R("hl", 14 + 2 * h + k, 15 + 2 * h + k))
-    qz(R("pl2c", 0, 128), R("pl2s", 0, 128), R("P2", 0, 512))
-    flags_times(0, 0, 7, "pl2c", "pl2s", 0)
-    act(R("xlt", 0, 32), bank(7, 32, 32), AF.Copy, bias=256.0 - 2 * BIG)
-    tt(R("xl0"), bank(7, 32), R("xlt", 0, 32), OP.add)
+    resets(R("rs4"), 32, 4, R("tab", 2048, 2176), -1.0)
+    ts(R("dw"), R("iob", 0, 32), col(11), OP.is_equal, 3.0, OP.mult)
+    lin(R("qm"), R("qn"))
+    fill(R("qm", 0, 64, 4), -500.0)
+    for d in range(2):
+        lin(R("gm2", d, 32, 2), gm)
+    lin(R("col2", 0, 1), col(1), 2.0)
+    ts(R("cof"), R("c44", 0, 2), R("col2", 0, 1), OP.add)
+    for h in range(2):
+        lin(R("UC", 32 * h + 1, 32 * h + 32, 4), R("gmt", 0, 24, 3), col(6 + h))
+    lin(R("UC", 3, 64, 4), gm, col(0))
+    ts(R("rep"), R("iob", 0, 16, 4), col(8), OP.add)
+    fill(R("c4"), 512.0 - 2 * BIG)
+    fill(R("c4", 2, 64, 4), 256.0)
+    fill(R("c4", 0, 64, 4), 512.0 - BIG)
+    lin(R("jl"), R("iob", 0, 16), 16.0, col(0))
+    tt(R("plx0"), ind(R("jl"), R("rep")), R("c4"), OP.add)
+    tt(R("plx1"), ind(R("plf"), R("rep")), R("c4"), OP.add)
+    lin(R("gth"), gm, 512.0 - 1e6, 1e6)
+    for e in range(4):
+        ts(R("ct0", e, 512, 4), R("rowb"), col(0), OP.is_equal, BIG, OP.mult)
+    qq("cq", 256, 128, R("ct0"))
+    for h in range(2):
+        lin(R("ns0", 128 * h, 128 * h + 128, 2), R("qn"), None, col(6 + h))
     pickout(R("et"), R("one"), 3, 4)
     for b in range(4):
-        qz(R("eqc", 128 * b, 128 * b + 128), R("eqs", 128 * b, 128 * b + 128), R("et", 3 - b, 515 - b))
-    own_parts("b0c", "b0s", 256)
-    fill(R("U0", 576, 640), 0.0)
-    choose(0, "b0c", "b0s")
-    merge(0, "b0c", "b0s", "b0c", "b0s", 256, 512)
-    decide(0)
-    for k in range(2):
-        cp(R("ln", 16 + k, 17 + k), R("lnf", 33 + 2 * lb - k, 34 + 2 * lb - k))
+        qq("eq", 128 * b, 128, R("et", 3 - b, 515 - b))
+    ahead(0, "b0")
+    choose(0, "b0", lambda h: R("P1", 512 + h, 768, 2))
+    qq("uq", 256, 128, R("P1", 256, 768))
+    mq(7, "cq", 0, "uq", 256)
+    final_list(0, 64)
     for h in range(2):
-        pick("b1c", "b1s", 256 + 128 * h, 384 + 128 * h, "b0c", "b0s", 0, 640 + 128 * h, R("ln", 8 * h, 8 * h + 8))
+        pick("b1", 256 + 128 * h, 384 + 128 * h, "b0", 0, 640 + 128 * h, R("ln", 8 * h, 8 * h + 8))
 
-    send_w("b1c", "b1s", "a1")
-    own_block("b1c", "b1s", "b0c", "b0s", 768, R("ln", 16, 18))
-    gram("b1c", "b1s", "b1c", "b1s", 256)
+    send_w("b1", "a1")
     for k in range(2):
-        act(R("fl", 16 * k, 16 * k + 16), R("z", k, 48, 3), AF.Sign, bias=-255.5)
-    ts(R("fl", 32, 48), bank(7, 16, 112), 128.0, OP.is_ge)
-    tt(R("fl", 48, 96), R("fl", 0, 48), R("gm"), OP.mult)
-    scan(R("fl", 96, 144), R("rs8"), R("fl", 48, 96), OP.mult, OP.add)
-    for k in range(2):
-        act(R("pen", k, 4, 2), R("fl", 103 + 16 * k, 112 + 16 * k, 8), AF.Copy, bias=128.0, scale=128.0)
-    tt(R("pen", 8, 12), R("pen", 0, 4), R("xi", 79, 128, 16), OP.max)
-    cp(R("xoa"), R("pen", 8, 12))
-    act(R("xd", 128, 258, 129), R("fl", 135, 144, 8), AF.Copy, scale=-1e29)
-    act(R("pen", 12, 16), R("fl", 103, 128, 8), AF.Copy, bias=16.0, scale=16.0)
-    act(R("pen", 16, 18), R("fl", 135, 144, 8), AF.Copy, scale=32.0)
-    local_scores(1)
-    pick("fc", "fs", 0, 256, "b1c", "b1s", 256, 512, R("pl"))
-    own_parts("fc", "fs", 0)
-    statics(1, [R("hl", 8, 9), R("hl", 9, 10)], 0)
-    weights(1, [R("hl", 18, 19), R("hl", 19, 20)], 10)
-    fill(R("P2", 640, 896), 0.0)
-    act(R("hls", 0, 4), R("hl", 4, 8), AF.Copy, scale=1.0 / 16)
-    act(R("hls", 4, 8), R("hl", 14, 18), AF.Copy, scale=1.0 / 256)
-    for e in range(2):
-        for k in range(2):
-            for h in range(2):
-                a = 640 + 128 * e + 64 * k
-                act(R("P2", a + h, a + 64, 4), R("nat", 32 + 16 * h, 48 + 16 * h), AF.Copy, scale=R("hls", 4 * e + 2 * h + k, 4 * e + 2 * h + k + 1))
-    qz(R("pl2c", 128, 256), R("pl2s", 128, 256), R("P2", 384, 896))
-    flags_times(1, 0, 7, "pl2c", "pl2s", 128)
-    act(R("xlt", 32, 64), bank(7, 32, 96), AF.Copy, bias=256.0 - 2 * BIG)
-    tt(R("xl1"), bank(7, 32, 64), R("xlt", 32, 64), OP.add)
-    fill(R("U1", 128, 320), 0.0)
-    sfill(R("U1", 576, 640), 0.0)
+        a = 4 * (2 * lb + 1 - k) + 3
+        cp(R("ln", 16 + k, 17 + k), (T.zs[:, a:a + 1], [("zs", 0, 64, 1)]))
+    pick("b1", 32 * lb, 32 * lb + 32, "b0", 0, 768, R("ln", 16, 18), True)
+    tt(R("fl", 0, 16), R("zs", 3, 64, 4), R("gth"), OP.is_ge)
+    scan(R("fl", 16, 32), R("rs8"), R("fl", 0, 16), OP.mult, OP.add)
+    tt(R("sm", 22, 24), R("sm", 18, 20), R("sm", 20, 22), OP.subtract)
+    tt(R("sm", 24, 26), R("fl", 23, 32, 8), R("sm", 22, 24), OP.mult)
+    for h in range(2):
+        ts(R("gg", 34 * h, 34 * h + 34, 33), R("qn", 1, 4, 2), R("sm", 24 + h, 25 + h), OP.is_equal, -1e29, OP.mult)
+    ts(R("xd", 128, 258, 129), R("sm", 24, 26), -3.0, OP.is_equal, -1e29, OP.mult)
+    local_scores(1, "b1", "b1", 256)
+    ts(R("sm", 26, 28), R("sm", 24, 26), -4.0, OP.is_le, 1.0, OP.add)
+    fill(R("U1", 0, 256), 0.0)
+    for h in range(2):
+        ts(R("U1", h, 256, 4), R("ns1", 128 * h, 128 * h + 128, 2), R("sm", 24 + h, 25 + h), OP.is_equal, R("sm", 26 + h, 27 + h), OP.mult)
+    fill(R("nlx", 2, 64, 4), -1.0)
     for k in range(3):
-        for h in range(2):
-            a = 128 + 64 * k
-            act(R("U1", a + h, a + 64, 4), R("nat", 32 + 16 * h, 48 + 16 * h), AF.Copy, scale=R("pen", 12 + 2 * k + h, 13 + 2 * k + h))
-    qz(R("qwc"), R("qws"), R("wt"))
-    choose(1, "b1c", "b1s")
-    cp(R("zb", 0, 16), bank(2, 16))
-    cp(R("zb", 16, 80), bank(3, 64, 16))
-    for k in (0, 1, 3, 4, 5):
-        a = 16 * k - (16 if k > 2 else 0)
-        tt(R("zp", 16 * k, 16 * k + 16), R("zb", a, a + 16), nl[k % 3], OP.add)
-    merge(1, "b1c", "b1s", "fc", "fs", 0, 256)
-    decide(1)
-    ts(R("zp", 160, 176), bank(7, 16, 112), 32.0, OP.mult)
-    tt(R("zp", 32, 48), R("zp", 160, 176), nl[2], OP.add)
-    for t in range(2):
-        a = 48 - 48 * t
-        tt(R("zp", 128 + 16 * t, 144 + 16 * t), R("zp", a, a + 16), R("zp", a + 16, a + 32), OP.max)
-        tt(R("zp", 96 + 16 * t, 112 + 16 * t), R("zp", 128 + 16 * t, 144 + 16 * t), R("zp", a + 32, a + 48), OP.max)
-    ts(R("fp", 0, 32), R("zp", 96, 128), -2 * BIG, OP.add, -1.0, OP.max)
-    tt(R("fp", 32, 64), R("fp", 0, 32), R("gm", 0, 32), OP.mult)
-    scan(R("fp", 64, 96), R("rs8", 0, 32), R("fp", 32, 64), OP.mult, OP.add)
-    for t in range(2):
-        for h in range(2):
-            a = 64 + 8 * (2 * t + h) + 7
-            dma("y", "st0", (T.pr[t:t + 1, 128 * h:128 * h + 128], []), R("fp", a, a + 1))
+        lin(R("nlx", (3, 1, 0)[k], 64, 4), nl[k], None, -BIG if k == 2 else -2 * BIG)
+    qq("qw", 0, 128, R("wt"))
+    ahead(1, "b1")
+    choose(1, "b1", lambda h: R("U1", 256 + h, 512, 2))
+    qq("uq", 384, 128, R("U1"))
+    mq(7, "cq", 128, "uq", 384)
+    final_list(1, 64)
     for h in range(2):
         a, b = 128 * h, 128 * h + 128
-        pick("oqc", "oqs", a, b, "fc", "fs", 0, 384 + 128 * h, R("ln", 20 + 8 * h, 28 + 8 * h))
+        pick("oq", a, b, "b1", 0, 768, R("ln", 20 + 8 * h, 28 + 8 * h))
         dma("y", "st0", (T.oc[:, 4 * a:4 * b], []), W8(R("oqc", a, b)))
-        mm(bank(4 + h, 128), R("qwc"), R("qws"), R("oqc", a, b), R("oqs", a, b))
+        mq(4 + h, "qw", 0, "oq", a)
+    for t in range(2):
+        tt(R("zp", 64 * t, 64 * t + 64), bank(7, 64, 64 * t), R("nlx"), OP.add)
+    scan(R("zq"), R("rs4"), R("zp"), OP.min, OP.max)
+    issue("v", lambda: g.vector.transpose(T.tp[0:32, :], T.zq[0:32, 3:128:4]), R("zq")[1], R("tp")[1], "qv", 1)
+    dma("y", "st0", (T.pr[:, :], []), (T.tp[0:32, 0:16], R("tp")[1]))
     for k in range(4):
         dma("s" if k % 2 else "y", "st0", (T.osc[4 * k:4 * k + 4, :], []), (T.oqs[32 * k:32 * k + 4, :], [("oqs", 0, 256, 1)]))
-    cp(R("ys", 0, 128), bank(4, 128))
-    act(R("ys", 128, 256), bank(5, 128))
     for h in range(2):
+        lin(R("ys", 128 * h, 128 * h + 128), bank(4 + h, 128))
         dma("y" if h == 0 else "s", "st0", (T.y[:, 128 * h:128 * h + 128], []), R("ys", 128 * h, 128 * h + 128))
 
     emit()

@@ -8,36 +8,36 @@ BIG = 4096.0
 RND = 1.5 * 2.0 ** 28
 FP8, U8, F32, BF, I32, U16 = "float8_e4m3fn_x4", "uint8", "float32", "bfloat16", "int32", "uint16"
 ORDER = """
-2 4 5 30 0 3 7 6 29 42 46 1 43 48 49 14 50 47 55 31 51 32 190 9 33 8 34 64 52 11 12 59 15 62 63 65 155 80 79 82 13 81 74 60 83 17 61 75 72 84 44 68 16 86 85 76 35 38 18 19 22 71 20 26 88 36 87 25 222 69 67 70 66 78 108 24 90 73 89 92 91 77 93 154 96 39 109 94 97 45 112 140 110 102 117 201 113 101 95 98 99 103 111 104 206 100 188 105 118 121 122 119 21 116 124 115 120 37 125 123 139 141 27 23 144 28 53 106 107 132 143 146 145 56 137 221 147 126 114 131 127 128 149 135 156 216 158 142 130 157 148 136 224 150 159 226 151 133 200 10 223 217 152 239 215 218 198 181 189 160 182 58 161 205 208 184 153 162 185 41 191 164 204 202 165 192 219 193 187 186 138 172 214 220 170 129 237 236 40 197 134 211 194 228 203 227 245 331 225 195 246 247 163 166 240 196 241 253 242 169 229 173 54 199 234 254 230 248 243 232 171 168 167 277 278 249 244 280 231 238 250 233 57 279 235 251 281 282 330 252 255 209 259 283 258 257 284 265 264 256 260 175 207 210 212 285 261 174 263 329 274 273 268 286 287 297 262 300 267 272 266 269 270 271 275 296 289 276 291 294 295 288 290 176 213 302 309 310 301 183 298 299 307 303 177 332 305 179 178 304 308 312 292 293 325 311 313 315 316 321 323 324 334 320 180 333 306 314 322 326 335 338 344 327 340 351 352 337 346 347 342 353 360 319 343 339 336 359 354 341 317 348 349 318 386 383 345 355 350 356 357 387 388 384 385 389 390 358 364 362 328 365 391 361 402 403 372 404 405 392 393 371 363 366 374 368 367 375 406 370 379 380 369 376 373 381 378 382 377 398 399 400 395 410 407 409 394 408 396 401 413 414 397 411 412
+30 41 3 0 2 1 5 6 7 43 42 58 59 45 29 47 48 46 150 49 51 44 32 31 60 55 61 4 74 75 76 77 37 137 36 78 33 56 50 79 210 80 67 62 57 63 81 65 54 190 82 83 8 11 103 13 10 19 9 12 17 14 66 68 34 64 85 52 73 70 71 86 84 87 113 89 72 91 92 88 90 35 135 149 194 94 93 69 96 97 112 104 116 106 105 114 211 193 108 98 99 16 18 15 23 27 95 20 26 24 100 101 22 25 21 110 138 111 119 115 139 117 120 102 141 126 118 38 40 136 134 218 142 107 109 121 183 39 128 129 127 130 131 151 122 153 169 144 53 219 221 143 220 224 225 123 140 145 222 226 223 146 170 148 195 147 171 124 196 152 197 125 177 154 155 198 156 178 132 172 157 229 212 231 237 133 216 213 227 235 233 179 181 180 159 160 166 163 165 182 168 167 214 199 248 184 185 239 186 158 247 215 228 249 174 176 240 187 241 188 191 161 268 269 244 242 261 262 250 251 246 234 259 217 256 205 230 270 263 264 164 28 162 265 189 192 243 232 245 266 201 271 272 255 252 273 209 258 267 274 253 284 257 254 236 276 238 328 206 200 204 325 278 282 202 208 275 279 280 277 281 331 173 207 285 286 260 287 283 288 290 289 175 308 291 301 299 296 300 293 309 295 298 302 304 303 324 306 307 297 311 310 327 332 312 326 315 314 320 318 321 319 322 329 323 335 341 333 337 338 350 357 305 349 358 342 334 339 336 347 345 343 344 351 313 359 352 292 294 371 372 373 354 378 379 380 360 361 356 362 374 381 353 316 317 382 375 365 368 366 355 203 340 383 384 376 377 346 385 348 386 387 388 330 389 390 391 369 394 367 363 364 395 396 392 393 397 370 398 404 407 408 403 406 405 400 412 413 399 401 414 409 410 411 418 415 419 402 416 417
 """
 ON = """
-0 1 2 6 7 8 9 10 11 12 15 16 17 18 19 20 21 22 23 24 25 26 27 28 30 31 32 33 34 35 36 37 38 39 40 41 42 43 44 45 46 47 48 49 50 51 52 53 54 56 57 58 60 61 62 64 65 66 68 69 71 72 73 74 75 76 77 80 82 83
+1 2 3 6 7 8 9 10 11 12 13 14 16 17 18 19 20 21 22 23 25 27 28 29 30 31 32 33 36 37 38 39 40 41 42 43 44 45 47 48 49 51 52 53 54 55 56 57 58 59 60 62 63 64 65 66 67 68 70 72 73 74 75 76 77 78 80 81 83 84 85 86 88 89 90 91 92 93 95
 """
 
 SCRATCH = {"nst": ("dram", [16, 138], I32)}
 for _t, _l in (
         (F32, "t48 48 k3 48 g24 48 j64 64 d8 8 ones 128 idn 128 col 12 gl48 48 own48 48 "
-              "jl 16 plf 16 dm 64 rs16 64 rs8 16 rs3 48 rs24 48 rs17 68 rs4 128 gmt 48 mk48 48 msk 8 dw 32 iv 32 xg 64 xg2 64 hl 32 hv 4 dif 16 dl 4 s4 4 sqa 128 "
-              "sel0 16 sel1 16 st 16 gm2 32 gd 32 c4 64 plx0 64 plx1 64 nlx 64 gs 512 gg 68 sc 68 sm 32 ma0 8 ma1 8 mx0 8 mx1 8 "
+              "plf 16 oh 128 dm 64 rs16 64 rs8 16 rs3 48 rs24 48 rs17 68 rs4 128 gmt 48 mk48 48 msk 8 dw 32 iv 32 xg 64 xg2 64 hl 20 hv 4 dif 10 sqa 128 "
+              "sel0 16 sel1 16 st 10 mid 20 gm4 64 gx 64 c4 64 plx0 64 plx1 64 nlx 64 gs 512 gg 68 sc 68 sm 32 ma0 8 ma1 8 mx0 8 mx1 8 "
               "tkc 18 xd 260 jk 260 jq 128 z 64 zs 64 zp 128 zq 128 tp 32 fl 32 ys 256 tab 2304"),
         (BF, "xt 1024 wt 512 iob 256 one 516 rowb 128 rowd 128 rowc 128 kr 256 krs 256 phb 2 et 516 pa 1024 P1 768 U1 512 UC 512 "
-             "posn 256 nr 512 qn 64 qm 64 ns0 256 ns1 256 ct0 512 ct1 512 nt 1024"),
+             "posn 256 nr 512 qn 64 qm 64 ns0 256 ns1 256 ct0 512 ct1 512 ntl 1024 ntn 1024 dh 1024 dk 1024"),
         (I32, "nbw 48 nn 138 hi 48 xi 160")):
     _w = _l.split()
     for _n, _k in zip(_w[0::2], _w[1::2]):
         SCRATCH[_n] = ("sbuf", [128, int(_k)], _t)
 PIECE = {}
 for _b, _t, _l in (
-        ("uu", U16, "ku 16 l18 18 o01 32 of4 4 xo 4 xp 4 ofx 8 lp 32 ln 36 pl 16 cof 2 rep 4"),
+        ("uu", U16, "ku 16 l18 18 o01 32 of4 4 xo 4 xp 4 ofx 8 lp 32 ln 36 pl 16 cof 4"),
         ("cn", I32, "pp 4 ci 12"),
-        ("fa", F32, "n2m 48 xa 48 kw 48 xm 48 kf 48 ks 48 km 48 kc 48 ss 2 ph 4 tkw 16 lo 2 wr 2"),
+        ("fa", F32, "n2m 48 xa 48 kw 48 xm 48 kf 48 ks 48 km 48 kc 48 ss 2 ph 4 lo 2 wr 2"),
         ("fb", F32, "m0 2 m1 2 col2 2 c44 4 gth 16")):
     _w, _c = _l.split(), 0
     for _n, _k in zip(_w[0::2], _w[1::2]):
         PIECE[_n] = (_b, _c, int(_k))
         _c += int(_k)
     SCRATCH[_b] = ("sbuf", [128, _c], _t)
-_w = "pa 256 pm 256 q0 256 qw 128 b0 768 b1 768 oq 256 eq 512 cq 384 uq 512 p0 256 p1 256".split()
+_w = "pa 256 pm 256 q0 256 qw 128 b0 1024 b1 1024 oq 256 eq 512 cq 384 uq 512".split()
 for _n, _k in zip(_w[0::2], _w[1::2]):
     SCRATCH[_n + "c"] = ("sbuf", [128, int(_k)], FP8)
     SCRATCH[_n + "s"] = ("sbuf", [128, int(_k)], U8)
@@ -183,6 +183,12 @@ def program(g, core, T, topo):
         else:
             ts(o, i, scale, OP.mult, bias, OP.add)
 
+    def relu(o, i, scale):
+        if scalar_turn():
+            act(o, i, AF.Relu, None, scale)
+        else:
+            ts(o, i, scale, OP.mult, 0.0, OP.max)
+
     def fill(o, c, fixed=False):
         if not fixed and scalar_turn():
             act(o, R("one", 0, width(o)), AF.Copy, scale=c)
@@ -207,6 +213,9 @@ def program(g, core, T, topo):
 
     def iota(o, pat, base, cm):
         issue("p", lambda: g.iota(o[0], pat, base, cm, allow_small_or_imprecise_dtypes=True), [], o[1], "qp", 1)
+
+    def pfill(o, c):
+        iota(o, [[0, width(o)]], int(c), 0)
 
     def resets(o, a, b, i=None, c=0.0):
         i = i or R("ones", 0, a * b)
@@ -251,8 +260,7 @@ def program(g, core, T, topo):
     iota(R("j64"), [[0, 4], [1, 16]], 0, 0)
     iota(R("d8"), [[0, 2], [32, 4]], 0, 0)
     iota(R("qn"), [[-16, 16], [-4, 2], [-1, 2]], -3, 0)
-    iota(R("c44", 0, 2), [[1, 2]], 10, 0)
-    iota(R("s4"), [[-128, 2], [0, 2]], 256, -1)
+    iota(R("c44"), [[2, 2], [0, 2]], 4, 0)
     fill(R("one", 0, 256), 1.0, True)
     scan(R("iob"), R("one", 0, 256), R("one", 0, 256), OP.add, OP.mult, -1.0)
     fill(R("one", 256, 516), 1.0, True)
@@ -264,36 +272,32 @@ def program(g, core, T, topo):
     def col(k):
         return R("col", k, k + 1)
     p0, p01 = R("pp", 0, 1), R("pp", 0, 2)
-    ts(c(3), R("pp", 2, 3), 15, OP.bitwise_and)
-    ts(col(9), c(3), 3.0, OP.mult, 2.0, OP.add)
-    ts(c(0), p0, 15, OP.bitwise_and)
+    ts(c(4), R("pp", 2, 3), 15, OP.bitwise_and)
+    ts(col(9), c(4), 3.0, OP.mult, 2.0, OP.add)
+    ts(c(5), p0, 15, OP.bitwise_and)
     ts(c(6, 2), p01, 240, OP.bitwise_and)
-    cp(col(3), c(3))
-    cp(R("col", 6, 8), R("ci", 6, 8))
+    cp(R("col", 4, 8), c(4, 4))
+    ts(c(0), p0, 2, OP.bitwise_and)
     ts(c(1), p0, 1, OP.bitwise_and)
     ts(c(2), p0, 96, OP.bitwise_and)
-    ts(c(8), p0, 15, OP.bitwise_and, 2, OP.arith_shift_right)
-    cp(col(0), c(0))
-    cp(R("col", 1, 3), R("ci", 1, 3))
-    cp(col(8), c(8))
-    lin(col(11), col(0), 2.0)
-    ts(R("mk48"), R("k3"), col(0), OP.add, col(9), OP.is_equal)
+    cp(R("col", 0, 3), c(0, 3))
+    lin(col(11), col(5), 2.0)
+    ts(R("mk48"), R("k3"), col(5), OP.add, col(9), OP.is_equal)
     ts(R("gmt"), R("g24"), col(6), OP.is_equal)
     gm = R("gmt", 0, 48, 3)
-    ts(R("rs3"), R("k3"), 0.0, OP.not_equal)
+    act(R("rs3"), R("k3"), AF.Sign)
     fill(R("rs24"), 1.0)
     fill(R("rs24", 0, 48, 24), 0.0)
-    lin(R("gl48"), R("t48"), None, col(3))
+    lin(R("gl48"), R("t48"), None, col(4))
     lin(R("own48"), R("gl48"), None, 256.0 * (1 - r))
     for b in range(7):
         lin(R("tab", 256 * b, 256 * b + 256), R("iob"), None, 256.0 * b)
     lin(R("rowc"), R("rowd"), None, -255.0)
     lin(R("tkc", 0, 16), R("iob", 0, 16), 32.0, RND - 64.0 * r)
-    ts(R("tkw"), R("iob", 0, 16), 2.0 * r, OP.is_lt, 512.0, OP.mult)
-    tt(R("tkc", 0, 16), R("tkc", 0, 16), R("tkw"), OP.add)
+    lin(R("tkc", 0, max(2 * r, 1)), R("iob", 0, max(2 * r, 1)), 32.0, RND - 64.0 * r + (512.0 if r else 0.0))
     for k in range(2):
         lin(R("tkc", 16 + k, 17 + k), R("iob", 2 * r + 1 - k, 2 * r + 2 - k), 32.0, RND)
-    nv = [col(6), col(3), col(7), col(3)]
+    nv = [col(6), col(4), col(7), col(4)]
 
     tt(R("n2m"), R("nbw"), R("mk48"), OP.mult)
     ts(R("hi"), R("nbw"), 1792, OP.bitwise_and)
@@ -323,7 +327,7 @@ def program(g, core, T, topo):
     mq(6, "pa", 0, "pm", 0)
     cp(R("l18"), bank(6, 18))
     qq("q0", 0, 256, R("xt"))
-    act(R("sqa"), R("rowb"), AF.Square, bias=col(3), scale=-1.0)
+    act(R("sqa"), R("rowb"), AF.Square, bias=col(4), scale=-1.0)
     for e in range(4):
         act(R("pa", 512 + e, 1024, 4), R("sqa"), AF.Relu, bias=1.0, scale=-1.0)
     qq("pa", 128, 128, R("pa", 512, 1024))
@@ -387,9 +391,9 @@ def program(g, core, T, topo):
         tt(x, ind(i, off), R("dm"), OP.mult)
         scan(o, R("rs16"), x, OP.mult, OP.add)
 
-    def decode(k0, s, a, start):
-        for h, b in k0:
-            mq(b + 3 * h, "eq", 128 * b, s, a + 128 * h, 128 if b else 256, start, not start)
+    def decode(s, a, start, stop):
+        for b in range(4):
+            mq(b, "eq", 128 * b, s, a, 256, start, stop)
 
     def local_scores(t, b, m, m0):
         for h in range(2):
@@ -408,48 +412,53 @@ def program(g, core, T, topo):
         rest = [(0, o), (o + 32, 128)] if 0 < o < 96 else [(32 - o // 3, 64), (64, 128 - o // 3)]
         for i, (lo, hi, to) in enumerate([(o, o + 16, o + 16), (o + 16, o + 32, o)] + [(lo, hi, lo) for lo, hi in rest]):
             dma("y", "lm%d" % t, (T[mx][to:to + hi - lo, lb:lb + 1], [(mx, 0, 8, 1)] if i == 0 else []), (T[ma][lo:hi, lb:lb + 1], [(ma, 0, 8, 1)]))
-        tt(R("sm", 0, 2), s0, s1, OP.is_ge)
+        for h in range(2):
+            ts(R("sm", h, h + 1), R("sc", 33 + 34 * h, 34 + 34 * h), R("sc", 16 + 34 * h, 17 + 34 * h), OP.is_ge, 0.5, OP.subtract)
 
     def ahead(t, b):
         sel, ct, ns = "sel%d" % t, "ct%d" % t, "ns%d" % t
+        decode(b, 256, True, True)
+        for e in range(4):
+            lin(R("dh", 256 * e, 256 * e + 256), bank(e, 256), 0.5)
+            lin(R("dk", 256 * e, 256 * e + 256), R("dh", 256 * e, 256 * e + 256))
+        decode(b, 256, True, False)
         for h in range(2):
-            lin(R("st", h, 16, 2), R("dif", h, 16, 2), R("sm", h, h + 1))
-        tt(R(sel), R("st"), R("hl", 0, 32, 2), OP.add)
-        tt(R("gd"), ind(R(sel), R("cof")), R("gm2"), OP.mult)
+            lin(R("st", h, 10, 2), R("dif", h, 10, 2), R("sm", h, h + 1))
+        tt(R(sel, 0, 10), R("st"), R("mid", 10, 20), OP.add)
         s = 2 * (1 - t)
         for h in range(2):
             ts(R(ct, 2 + h, 512, 4), R("rowb"), R(sel, 4 + s + h, 5 + s + h), OP.is_equal, BIG, OP.mult)
             lin(R(ns, 128 * h + 1, 128 * h + 128, 2), R("qm"), None, R(sel, s + h, s + h + 1))
         qq("cq", 128 * t, 128, R(ct))
-        decode(((0, 0), (0, 1), (0, 2), (0, 3)), b, 256, True)
+        for h in range(2):
+            relu(R("UC", 32 * h, 32 * h + 32), R("gx", 32 * h, 32 * h + 32), R("sm", h, h + 1))
+        qq("uq", 128 * t, 128, R("UC"))
+        mq(6, "cq", 256, "uq", 128 * t)
+        ts(R("lp", 16 * t, 16 * t + 16), bank(6, 16), 1.0 / BIG, OP.mult)
+        for h in range(2):
+            for e in range(4):
+                tt(R("ntl", 512 * h + e, 512 * h + 512, 4), ind(R("dh", 256 * e, 256 * e + 256), R("lp", 16 * t + 8 * h, 16 * t + 8 * h + 8)),
+                   R("dk", 256 * e + 128 * h, 256 * e + 128 * h + 128), OP.add)
+        qq(b, 512, 256, R("ntl"))
 
     def choose(t, b, u):
-        mx, m, p = "mx%d" % t, "m%d" % t, "p%d" % t
+        mx, m = "mx%d" % t, "m%d" % t
         arrive("a%d" % t, b + "c", 0, 256)
         arrive("a%d" % t, b + "s", 0, 256)
+        arrive("e%d" % t, mx, 0, 8)
         for h in range(2):
             mq(4 + h, b, 256 + 128 * h, b, 128 * h)
             tt(R("xd", 129 * h, 129 * h + 128), bank(4 + h, 128), R("idn"), OP.mult)
             total(R("sm", 16 + h, 17 + h), R("xd", 129 * h, 129 * h + 128 + t), R("jk", 130 * h, 130 * h + 128 + t))
             ts(R("sm", 18 + h, 19 + h), R(m, h, h + 1), R("sm", 16 + h, 17 + h), OP.is_ge, R("sel%d" % t, 8 + h, 9 + h), OP.mult)
-            ts(R("UC", 32 * h, 32 * h + 32, 2), R("gd", 16 * h, 16 * h + 16), R("sm", 18 + h, 19 + h), OP.mult, R("sel%d" % t, 14 + h, 15 + h), OP.mult)
-        qq("uq", 128 * t, 128, R("UC"))
-        mq(6, "cq", 256, "uq", 128 * t)
-        ts(R("lp", 16 * t, 16 * t + 16), bank(6, 16), 1.0 / BIG, OP.mult)
-        decode(((1, 1), (1, 2), (1, 3)), b, 256, True)
-        for h in range(2):
-            pick(p, 128 * h, 128 * h + 128, b, 0, 512, R("lp", 16 * t + 8 * h, 16 * t + 8 * h + 8))
-        decode(((0, 1), (0, 2), (0, 0), (0, 3), (1, 1), (1, 2), (1, 3)), p, 0, False)
-        for h in range(2):
-            for e in range(4):
-                lin(R("nt", 512 * h + e, 512 * h + 512, 4), bank(e + 3 * h, 128) if e else bank(0, 128, 128 * h), 0.5)
-            qq(b, 512 + 128 * h, 128, R("nt", 512 * h, 512 * h + 512))
-        arrive("e%d" % t, mx, 0, 8)
-        for h in range(2):
             ts(R("ofx", 4 * h, 4 * h + 4), R(mx, 4 * h, 4 * h + 4), R("sm", 16 + h, 17 + h), OP.is_ge, col(11), OP.add)
             act(R("jq", 64 * h, 64 * h + 64), ind(R("dw"), R("ofx", 4 * h, 4 * h + 4)), AF.Relu, bias=R("sm", 18 + h, 19 + h),
                 accum=R("sm", 20 + h, 21 + h))
             ts(u(h), R("ns%d" % t, 128 * h, 128 * h + 128), R("sm", 20 + h, 21 + h), OP.add, R("sm", 18 + h, 19 + h), OP.is_equal)
+        decode(b, 0, False, True)
+        for e in range(4):
+            lin(R("ntn", e, 1024, 4), bank(e, 256), 0.5)
+        qq(b, 768, 256, R("ntn"))
 
     def final_list(t, a):
         tt(R("z"), bank(7, 64, a), R("plx%d" % t), OP.add)
@@ -462,7 +471,7 @@ def program(g, core, T, topo):
     resets(R("rs8"), 2, 8)
     resets(R("rs16"), 4, 16)
     resets(R("rs17"), 4, 17)
-    ts(R("dm"), R("j64"), col(0), OP.is_equal)
+    ts(R("dm"), R("j64"), col(5), OP.is_equal)
     for a in range(2):
         ts(R("o01", 16 * a, 16 * a + 16), nl[1 - a], -256.0 * r, OP.add)
     act(R("nr"), ind(R("iob"), R("o01")))
@@ -489,36 +498,30 @@ def program(g, core, T, topo):
     ts(R("xi", 136, 144), R("xi", 15, 128, 16), 240, OP.bitwise_and)
     ts(R("xi", 144, 152), R("xi", 15, 128, 16), 15, OP.bitwise_and)
     cp(R("hl", 0, 16), R("xi", 136, 152))
-    fill(R("hl", 16, 20, 2), -4.0)
-    fill(R("hl", 17, 20, 2), -8.0)
-    fill(R("hl", 28, 32, 2), -0.25)
-    fill(R("hl", 29, 32, 2), -0.125)
-    tt(R("dl", 0, 4), R("xi", 79, 128, 16), R("s4"), OP.add)
-    ts(R("hl", 20, 24), R("dl"), RND, OP.add, -RND, OP.add)
-    tt(R("hl", 24, 28), R("dl"), R("hl", 20, 24), OP.subtract)
-    tt(R("dif"), R("hl", 1, 32, 2), R("hl", 0, 32, 2), OP.subtract)
+    pfill(R("hl", 16, 20, 2), -4.0)
+    pfill(R("hl", 17, 20, 2), -8.0)
+    tt(R("dif"), R("hl", 1, 20, 2), R("hl", 0, 20, 2), OP.subtract)
+    tt(R("mid", 0, 10), R("hl", 1, 20, 2), R("hl", 0, 20, 2), OP.add)
+    lin(R("mid", 10, 20), R("mid", 0, 10), 0.5)
     pickout(R("idn"), R("ones"), 0, 1)
     resets(R("rs4"), 32, 4, R("tab", 2048, 2176), -1.0)
     ts(R("dw"), R("iob", 0, 32), col(11), OP.is_equal, 3.0, OP.mult)
-    lin(R("qm"), R("qn"))
-    fill(R("qm", 0, 64, 4), -500.0)
-    for d in range(2):
-        lin(R("gm2", d, 32, 2), gm)
-    lin(R("col2", 0, 1), col(1), 2.0)
-    ts(R("cof"), R("c44", 0, 2), R("col2", 0, 1), OP.add)
-    for h in range(2):
-        lin(R("UC", 32 * h + 1, 32 * h + 32, 4), R("gmt", 0, 24, 3), col(6 + h))
-    lin(R("UC", 3, 64, 4), gm, col(0))
-    ts(R("rep"), R("iob", 0, 16, 4), col(8), OP.add)
-    fill(R("c4"), 512.0 - 2 * BIG)
-    fill(R("c4", 2, 64, 4), 256.0)
-    fill(R("c4", 0, 64, 4), 512.0 - BIG)
-    lin(R("jl"), R("iob", 0, 16), 16.0, col(0))
-    tt(R("plx0"), ind(R("jl"), R("rep")), R("c4"), OP.add)
-    tt(R("plx1"), ind(R("plf"), R("rep")), R("c4"), OP.add)
-    lin(R("gth"), gm, 512.0 - 1e6, 1e6)
+    iota(R("qm"), [[-16, 16], [-4, 2], [-1, 2]], -3, 0)
+    pfill(R("qm", 0, 64, 4), -500.0)
     for e in range(4):
-        ts(R("ct0", e, 512, 4), R("rowb"), col(0), OP.is_equal, BIG, OP.mult)
+        lin(R("gm4", e, 64, 4), gm, 2.0 if e % 2 else -2.0)
+    lin(R("col2", 0, 1), col(0), 4.0, col(1))
+    ts(R("cof"), R("c44"), R("col2", 0, 1), OP.add)
+    tt(R("gx"), ind(R("hl", 0, 16), R("cof")), R("gm4"), OP.mult)
+    c4 = (768.0 - BIG, 512.0 - 2 * BIG, 256.0, 512.0 - 2 * BIG)
+    for k in range(4):
+        iota(R("c4", k, 64, 4), [[16, 16]], int(c4[k]), 0)
+        lin(R("plx1", k, 64, 4), R("plf"), None, c4[k])
+    lin(R("plx0"), R("c4"), None, col(5))
+    lin(R("gth"), gm, 512.0 - 1e6, 1e6)
+    ts(R("oh"), R("rowb"), col(5), OP.is_equal, BIG, OP.mult)
+    for e in range(4):
+        lin(R("ct0", e, 512, 4), R("oh"))
     qq("cq", 256, 128, R("ct0"))
     for h in range(2):
         lin(R("ns0", 128 * h, 128 * h + 128, 2), R("qn"), None, col(6 + h))
@@ -530,14 +533,13 @@ def program(g, core, T, topo):
     qq("uq", 256, 128, R("P1", 256, 768))
     mq(7, "cq", 0, "uq", 256)
     final_list(0, 64)
-    for h in range(2):
-        pick("b1", 256 + 128 * h, 384 + 128 * h, "b0", 0, 640 + 128 * h, R("ln", 8 * h, 8 * h + 8))
+    pick("b1", 256, 512, "b0", 0, 1024, R("ln", 0, 16))
 
     send_w("b1", "a1")
     for k in range(2):
         a = 4 * (2 * lb + 1 - k) + 3
         cp(R("ln", 16 + k, 17 + k), (T.zs[:, a:a + 1], [("zs", 0, 64, 1)]))
-    pick("b1", 32 * lb, 32 * lb + 32, "b0", 0, 768, R("ln", 16, 18), True)
+    pick("b1", 32 * lb, 32 * lb + 32, "b0", 0, 1024, R("ln", 16, 18), True)
     tt(R("fl", 0, 16), R("zs", 3, 64, 4), R("gth"), OP.is_ge)
     scan(R("fl", 16, 32), R("rs8"), R("fl", 0, 16), OP.mult, OP.add)
     tt(R("sm", 22, 24), R("sm", 18, 20), R("sm", 20, 22), OP.subtract)
@@ -547,10 +549,10 @@ def program(g, core, T, topo):
     ts(R("xd", 128, 258, 129), R("sm", 24, 26), -3.0, OP.is_equal, -1e29, OP.mult)
     local_scores(1, "b1", "b1", 256)
     ts(R("sm", 26, 28), R("sm", 24, 26), -4.0, OP.is_le, 1.0, OP.add)
-    fill(R("U1", 0, 256), 0.0)
+    pfill(R("U1", 0, 256), 0.0)
     for h in range(2):
         ts(R("U1", h, 256, 4), R("ns1", 128 * h, 128 * h + 128, 2), R("sm", 24 + h, 25 + h), OP.is_equal, R("sm", 26 + h, 27 + h), OP.mult)
-    fill(R("nlx", 2, 64, 4), -1.0)
+    pfill(R("nlx", 2, 64, 4), -1.0)
     for k in range(3):
         lin(R("nlx", (3, 1, 0)[k], 64, 4), nl[k], None, -BIG if k == 2 else -2 * BIG)
     qq("qw", 0, 128, R("wt"))
@@ -561,7 +563,7 @@ def program(g, core, T, topo):
     final_list(1, 64)
     for h in range(2):
         a, b = 128 * h, 128 * h + 128
-        pick("oq", a, b, "b1", 0, 768, R("ln", 20 + 8 * h, 28 + 8 * h))
+        pick("oq", a, b, "b1", 0, 1024, R("ln", 20 + 8 * h, 28 + 8 * h))
         dma("y", "st0", (T.oc[:, 4 * a:4 * b], []), W8(R("oqc", a, b)))
         mq(4 + h, "qw", 0, "oq", a)
     for t in range(2):

import math
from concourse.bass import DstId, RemoteDMATransfer
from concourse.mybir import dt, AluOpType, AxisListType, ActivationFunctionType

OP = AluOpType
AF = ActivationFunctionType
BIG = 4096.0
RND = 1.5 * 2.0 ** 28
FP8, U8, F32, BF, I32, U16 = "float8_e4m3fn_x4", "uint8", "float32", "bfloat16", "int32", "uint16"
ORDER = """
30 41 3 0 2 1 5 6 7 43 42 58 59 45 29 47 48 46 150 49 51 44 32 31 60 55 61 4 74 75 76 77 37 137 36 78 33 56 50 79 210 80 67 62 57 63 81 65 54 190 82 83 8 11 103 13 10 19 9 12 17 14 66 68 34 64 85 52 73 70 71 86 84 87 113 89 72 91 92 88 90 35 135 149 194 94 93 69 96 97 112 104 116 106 105 114 211 193 108 98 99 16 18 15 23 27 95 20 26 24 100 101 22 25 21 110 138 111 119 115 139 117 120 102 141 126 118 38 40 136 134 218 142 107 109 121 183 39 128 129 127 130 131 151 122 153 169 144 53 219 221 143 220 224 225 123 140 145 222 226 223 146 170 148 195 147 171 124 196 152 197 125 177 154 155 198 156 178 132 172 157 229 212 231 237 133 216 213 227 235 233 179 181 180 159 160 166 163 165 182 168 167 214 199 248 184 185 239 186 158 247 215 228 249 174 176 240 187 241 188 191 161 268 269 244 242 261 262 250 251 246 234 259 217 256 205 230 270 263 264 164 28 162 265 189 192 243 232 245 266 201 271 272 255 252 273 209 258 267 274 253 284 257 254 236 276 238 328 206 200 204 325 278 282 202 208 275 279 280 277 281 331 173 207 285 286 260 287 283 288 290 289 175 308 291 301 299 296 300 293 309 295 298 302 304 303 324 306 307 297 311 310 327 332 312 326 315 314 320 318 321 319 322 329 323 335 341 333 337 338 350 357 305 349 358 342 334 339 336 347 345 343 344 351 313 359 352 292 294 371 372 373 354 378 379 380 360 361 356 362 374 381 353 316 317 382 375 365 368 366 355 203 340 383 384 376 377 346 385 348 386 387 388 330 389 390 391 369 394 367 363 364 395 396 392 393 397 370 398 404 407 408 403 406 405 400 412 413 399 401 414 409 410 411 418 415 419 402 416 417
"""
ON = """
1 2 3 6 7 8 9 10 11 12 13 14 16 17 18 19 20 21 22 23 25 27 28 29 30 31 32 33 36 37 38 39 40 41 42 43 44 45 47 48 49 51 52 53 54 55 56 57 58 59 60 62 63 64 65 66 67 68 70 72 73 74 75 76 77 78 80 81 83 84 85 86 88 89 90 91 92 93 95
"""

SCRATCH = {"nst": ("dram", [16, 138], I32)}
for _t, _l in (
        (F32, "t48 48 k3 48 g24 48 j64 64 d8 8 ones 128 idn 128 col 12 gl48 48 own48 48 "
              "plf 16 oh 128 dm 64 rs16 64 rs8 16 rs3 48 rs24 48 rs17 68 rs4 128 gmt 48 mk48 48 msk 8 dw 32 iv 32 xg 64 xg2 64 hl 20 hv 4 dif 10 sqa 128 "
              "sel0 16 sel1 16 st 10 mid 20 gm4 64 gx 64 c4 64 plx0 64 plx1 64 nlx 64 gs 512 gg 68 sc 68 sm 32 ma0 8 ma1 8 mx0 8 mx1 8 "
              "tkc 18 xd 260 jk 260 jq 128 z 64 zs 64 zp 128 zq 128 tp 32 fl 32 ys 256 tab 2304"),
        (BF, "xt 1024 wt 512 iob 256 one 516 rowb 128 rowd 128 rowc 128 kr 256 krs 256 phb 2 et 516 pa 1024 P1 768 U1 512 UC 512 "
             "posn 256 nr 512 qn 64 qm 64 ns0 256 ns1 256 ct0 512 ct1 512 ntl 1024 ntn 1024 dh 1024 dk 1024"),
        (I32, "nbw 48 nn 138 hi 48 xi 160")):
    _w = _l.split()
    for _n, _k in zip(_w[0::2], _w[1::2]):
        SCRATCH[_n] = ("sbuf", [128, int(_k)], _t)
PIECE = {}
for _b, _t, _l in (
        ("uu", U16, "ku 16 l18 18 o01 32 of4 4 xo 4 xp 4 ofx 8 lp 32 ln 36 pl 16 cof 4"),
        ("cn", I32, "pp 4 ci 12"),
        ("fa", F32, "n2m 48 xa 48 kw 48 xm 48 kf 48 ks 48 km 48 kc 48 ss 2 ph 4 lo 2 wr 2"),
        ("fb", F32, "m0 2 m1 2 col2 2 c44 4 gth 16")):
    _w, _c = _l.split(), 0
    for _n, _k in zip(_w[0::2], _w[1::2]):
        PIECE[_n] = (_b, _c, int(_k))
        _c += int(_k)
    SCRATCH[_b] = ("sbuf", [128, _c], _t)
_w = "pa 256 pm 256 q0 256 qw 128 b0 1024 b1 1024 oq 256 eq 512 cq 384 uq 512".split()
for _n, _k in zip(_w[0::2], _w[1::2]):
    SCRATCH[_n + "c"] = ("sbuf", [128, int(_k)], FP8)
    SCRATCH[_n + "s"] = ("sbuf", [128, int(_k)], U8)
for _k in range(8):
    SCRATCH["bk%d" % _k] = ("psum", [128, 512], F32)

SEMAPHORES = ["qv", "qs", "qt", "qp", "lnb", "lx", "lx2", "lx3", "lw", "lst", "lnn", "st0", "lm0", "lm1", "loc", "a0", "a1", "e0", "e1"]


def program(g, core, T, topo):
    r = T.rank_of(core)
    blk = [(r + q) % 8 for q in range(8)]
    lb = blk[r]
    Q = {"v": g.vector, "s": g.scalar, "t": g.tensor, "y": g.sync, "p": g}
    cnt = {}
    known = {k: {} for k in Q}
    acc = {}
    ops = []
    group = {}
    on_scalar = set(int(k) for k in ON.split())
    either_n = [0]

    def meet(a, b):
        return a[0] < b[1] and b[0] < a[1] and (a[0] - b[0]) % math.gcd(a[2], b[2]) == 0

    def issue(q, fn, reads, writes, sem, n):
        deps, me = set(), len(ops)
        for w, regs in ((False, reads), (True, writes)):
            for b, lo, hi, st in regs:
                for a in acc.get(b, []):
                    if (w or a[3] or (b[:2] == "bk" and ops[a[4]][0] != q)) and meet((lo, hi, st), a):
                        deps.update(group.get(ops[a[4]][3], [a[4]]))
        ops.append([q, fn, sorted(deps), sem, n])
        if n != 1:
            group.setdefault(sem, []).append(me)
        for w, regs in ((False, reads), (True, writes)):
            for b, lo, hi, st in regs:
                l = acc.setdefault(b, [])
                if w and st == 1:
                    l[:] = [a for a in l if not (lo <= a[0] and a[1] <= hi)]
                l.append((lo, hi, st, w, me))
        return me

    def emit():
        total = {m: sum(ops[i][4] for i in l) for m, l in group.items()}
        count, clock = [0] * len(ops), [None] * len(ops)
        for i in ([int(k) for k in ORDER.split()] or range(len(ops))):
            q, fn, deps, sem, n = ops[i][:5]
            if q == "a":
                count[i], clock[i] = n, {}
                continue
            kn = known[q]
            for d in sorted(deps, key=lambda d: -count[d]):
                if not ops[d][3] or (q == "t" and ops[d][0] == "t"):
                    continue
                m = ops[d][3]
                c = total.get(m, count[d])
                if kn.get(m, 0) < c:
                    Q[q].wait_ge(T.sem[m], c)
                    kn[m] = c
                for k, v in clock[d].items():
                    kn[k] = max(kn.get(k, 0), v)
            ins = fn()
            if sem:
                ins.then_inc(T.sem[sem], n)
                cnt[sem] = cnt.get(sem, 0) + n
                count[i] = cnt[sem]
            clock[i] = dict(kn)

    def R(n, a=0, b=None, s=1):
        n, base, w = PIECE.get(n, (n, 0, SCRATCH[n][1][1] if n in SCRATCH else 0))
        a, b = base + a, base + (w if b is None else b)
        ap = T[n][:, slice(a, b) if s == 1 else slice(a, b, s)]
        if SCRATCH[n][0] == "psum":
            return ap, [(n, 0, 512, 1)]
        return ap, [(n, a, b, s)]

    def W32(v):
        return v[0].bitcast(dt.uint32), v[1]

    def W8(v):
        return v[0].bitcast(dt.uint8), v[1]

    def ind(win, off):
        return win[0].indirect(off[0]), win[1] + off[1]

    def val(s):
        return (s[0], s[1]) if isinstance(s, tuple) else (s, [])

    def width(v):
        r0 = v[1][0]
        return -(-(r0[2] - r0[1]) // r0[3])

    def ts(o, i, s1, op0, s2=None, op1=None):
        a, b = val(s1), val(s2)
        rd = i[1] + a[1] + b[1]
        if op1 is None:
            issue("v", lambda: g.vector.tensor_scalar(o[0], i[0], a[0], None, op0), rd, o[1], "qv", 1)
        else:
            issue("v", lambda: g.vector.tensor_scalar(o[0], i[0], a[0], b[0], op0, op1), rd, o[1], "qv", 1)

    def tt(o, a, b, op):
        issue("v", lambda: g.vector.tensor_tensor(o[0], a[0], b[0], op), a[1] + b[1], o[1], "qv", 1)

    def cp(o, i):
        issue("v", lambda: g.vector.tensor_copy(o[0], i[0]), i[1], o[1], "qv", 1)

    def red(o, i):
        issue("v", lambda: g.vector.tensor_reduce(o[0], i[0], AxisListType.X, OP.add), i[1], o[1], "qv", 1)

    def scan(o, a, b, op0, op1, init=0.0):
        issue("v", lambda: g.vector.tensor_tensor_scan(o[0], a[0], b[0], init, op0, op1), a[1] + b[1], o[1], "qv", 1)

    def qz(c, s, i):
        issue("v", lambda: g.vector.quantize_mx(c[0], s[0], i[0]), i[1], c[1] + s[1], "qv", 1)

    def act(o, i, f=AF.Copy, bias=None, scale=None, accum=None):
        kw, rd, wr = {}, list(i[1]), list(o[1])
        if bias is not None:
            kw["bias"] = val(bias)[0]
            rd += val(bias)[1]
        if scale is not None:
            kw["scale"] = val(scale)[0]
            rd += val(scale)[1]
        if accum is not None:
            kw["accum_out"] = accum[0]
            wr += accum[1]
        issue("s", lambda: g.scalar.activation(o[0], i[0], f, **kw), rd, wr, "qs", 1)

    def scalar_turn():
        either_n[0] += 1
        return either_n[0] - 1 in on_scalar

    def lin(o, i, scale=None, bias=None):
        if scalar_turn():
            act(o, i, AF.Identity if isinstance(bias, tuple) else AF.Copy, bias, scale)
        elif scale is None and bias is None:
            cp(o, i)
        elif bias is None:
            ts(o, i, scale, OP.mult)
        elif scale is None:
            ts(o, i, bias, OP.add)
        else:
            ts(o, i, scale, OP.mult, bias, OP.add)

    def relu(o, i, scale):
        if scalar_turn():
            act(o, i, AF.Relu, None, scale)
        else:
            ts(o, i, scale, OP.mult, 0.0, OP.max)

    def fill(o, c, fixed=False):
        if not fixed and scalar_turn():
            act(o, R("one", 0, width(o)), AF.Copy, scale=c)
        else:
            issue("v", lambda: g.vector.memset(o[0], c), [], o[1], "qv", 1)

    def total(o, x, junk):
        if scalar_turn():
            act(junk, x, AF.Identity, accum=o)
        else:
            red(o, x)

    def mm(o, lc, ls, rc, rs, start=True, stop=True):
        issue("t", lambda: g.tensor.matmul_mx(o[0], lc[0], ls[0], rc[0], rs[0], start, stop),
              lc[1] + ls[1] + rc[1] + rs[1], o[1], "qt", 1)

    def mq(o, l, a, m, b, n=128, start=True, stop=True):
        mm(R("bk%d" % o, 0, n), R(l + "c", a, a + 128), R(l + "s", a, a + 128), R(m + "c", b, b + n), R(m + "s", b, b + n), start, stop)

    def qq(d, a, n, i):
        qz(R(d + "c", a, a + n), R(d + "s", a, a + n), i)

    def iota(o, pat, base, cm):
        issue("p", lambda: g.iota(o[0], pat, base, cm, allow_small_or_imprecise_dtypes=True), [], o[1], "qp", 1)

    def pfill(o, c):
        iota(o, [[0, width(o)]], int(c), 0)

    def resets(o, a, b, i=None, c=0.0):
        i = i or R("ones", 0, a * b)
        issue("p", lambda: g.affine_select(o[0], i[0], [[0, a], [1, b]], OP.not_equal, c, 0, 0), i[1], o[1], "qp", 1)

    def pickout(o, i, base, cm):
        issue("p", lambda: g.affine_select(o[0], i[0], [[-1, width(o)]], OP.is_equal, 0.0, base, cm), i[1], o[1], "qp", 1)

    def dma(q, sem, out, i):
        issue(q, lambda: Q[q].dma_start(out[0], i[0]), i[1], out[1], sem, 16)

    def bank(k, n, a=0):
        return R("bk%d" % k, a, a + n)

    for gr in range(8):
        dma("ys"[gr % 2], "lnb", (T.nbw[16 * gr:16 * gr + 16, :], [("nbw", 0, 48, 1)] if gr == 0 else []), (T.nb[:, :], []))
    dma("y", "lx", R("xt"), (T.x[:, :], []))
    dma("y", "lx2", R("P1", 72, 512), (T.x[:, 0:440], []))
    dma("y", "lx3", R("UC", 64, 512), (T.x[:, 0:448], []))
    first = True
    for k in range(3):
        i = 0
        while i < 16:
            a, o = (3 * i + k) % 16, (3 * i + k) // 16
            n = min((15 - a) // 3 + 1, 16 - i)
            dma("y", "lst", (T.nst[i:i + n, 46 * k:46 * k + 46], [("nst", 0, 138, 1)] if first else []),
                (T.nb[a:a + 3 * (n - 1) + 1:3, o:o + 46], []))
            i, first = i + n, False
    for gr in range(8):
        dma("y", "lnn", (T.nn[16 * gr:16 * gr + 16, :], [("nn", 0, 138, 1)] if gr == 0 else []), (T.nst[:, :], [("nst", 0, 138, 1)]))
    dma("y", "lw", R("wt"), (T.w[:, :], []))
    nl = [R("nn", 46 * k, 46 * k + 46, 3) for k in range(3)]

    iota(R("pp", 0, 2), [[128, 2]], 0, 1)
    iota(R("pp", 2, 3), [[0, 1]], 10, 11)
    iota(R("k3"), [[0, 16], [16, 3]], 0, 0)
    iota(R("t48"), [[16, 16], [0, 3]], 256 * r, 0)
    iota(R("g24"), [[0, 2], [16, 8], [0, 3]], 0, 0)
    iota(R("tab", 1792, 2304), [[1, 512]], 1792, 0)
    iota(R("rowd"), [[0, 8], [2, 16]], 0, 0)
    iota(R("rowb"), [[0, 8], [1, 16]], 0, 0)
    iota(R("j64"), [[0, 4], [1, 16]], 0, 0)
    iota(R("d8"), [[0, 2], [32, 4]], 0, 0)
    iota(R("qn"), [[-16, 16], [-4, 2], [-1, 2]], -3, 0)
    iota(R("c44"), [[2, 2], [0, 2]], 4, 0)
    fill(R("one", 0, 256), 1.0, True)
    scan(R("iob"), R("one", 0, 256), R("one", 0, 256), OP.add, OP.mult, -1.0)
    fill(R("one", 256, 516), 1.0, True)
    lin(R("ones"), R("one", 0, 128))

    def c(k, n=1):
        return R("ci", k, k + n)

    def col(k):
        return R("col", k, k + 1)
    p0, p01 = R("pp", 0, 1), R("pp", 0, 2)
    ts(c(4), R("pp", 2, 3), 15, OP.bitwise_and)
    ts(col(9), c(4), 3.0, OP.mult, 2.0, OP.add)
    ts(c(5), p0, 15, OP.bitwise_and)
    ts(c(6, 2), p01, 240, OP.bitwise_and)
    cp(R("col", 4, 8), c(4, 4))
    ts(c(0), p0, 2, OP.bitwise_and)
    ts(c(1), p0, 1, OP.bitwise_and)
    ts(c(2), p0, 96, OP.bitwise_and)
    cp(R("col", 0, 3), c(0, 3))
    lin(col(11), col(5), 2.0)
    ts(R("mk48"), R("k3"), col(5), OP.add, col(9), OP.is_equal)
    ts(R("gmt"), R("g24"), col(6), OP.is_equal)
    gm = R("gmt", 0, 48, 3)
    act(R("rs3"), R("k3"), AF.Sign)
    fill(R("rs24"), 1.0)
    fill(R("rs24", 0, 48, 24), 0.0)
    lin(R("gl48"), R("t48"), None, col(4))
    lin(R("own48"), R("gl48"), None, 256.0 * (1 - r))
    for b in range(7):
        lin(R("tab", 256 * b, 256 * b + 256), R("iob"), None, 256.0 * b)
    lin(R("rowc"), R("rowd"), None, -255.0)
    lin(R("tkc", 0, 16), R("iob", 0, 16), 32.0, RND - 64.0 * r)
    lin(R("tkc", 0, max(2 * r, 1)), R("iob", 0, max(2 * r, 1)), 32.0, RND - 64.0 * r + (512.0 if r else 0.0))
    for k in range(2):
        lin(R("tkc", 16 + k, 17 + k), R("iob", 2 * r + 1 - k, 2 * r + 2 - k), 32.0, RND)
    nv = [col(6), col(4), col(7), col(4)]

    tt(R("n2m"), R("nbw"), R("mk48"), OP.mult)
    ts(R("hi"), R("nbw"), 1792, OP.bitwise_and)
    tt(R("kw"), R("n2m"), R("gl48"), OP.is_gt)
    tt(R("xa"), R("hi"), R("own48"), OP.add)
    tt(R("xm"), R("kw"), R("xa"), OP.mult)
    tt(R("kf"), R("n2m"), R("xm"), OP.max)
    tt(R("km"), R("kf"), R("gmt"), OP.mult)
    scan(R("ks"), R("rs3"), R("kf"), OP.mult, OP.add)
    scan(R("kc"), R("rs24"), R("km"), OP.mult, OP.add)
    cp(R("ku"), R("ks", 2, 48, 3))
    act(R("jk", 0, 256), ind(R("tab"), R("ku")), AF.Sign, bias=R("kc", 23, 24), scale=-1.0, accum=R("ss", 0, 1))
    ts(R("kr"), ind(R("tab"), R("ku")), R("kc", 47, 48), OP.is_lt, 2.0, OP.mult)
    scan(R("krs"), R("kr"), R("kr"), OP.add, OP.max)
    p2 = [R("ss", 0, 1), R("krs", 255, 256)]
    rw = [R("rowc"), R("rowd")]
    hi2 = [R("ph", 2, 3), R("phb", 0, 1)]
    for h in range(2):
        ts(R("ph", h, h + 1), p2[h], -15.0 if h else 240.0, OP.add, RND, OP.add)
        ts(hi2[h], R("ph", h, h + 1), -RND, OP.add)
    for e in range(4):
        ts(R("P1", e, 72, 4), R("tkc"), R("ph", e // 2, e // 2 + 1), OP.is_equal, nv[e], OP.mult)
    qq("pm", 0, 128, R("P1", 0, 512))
    for e in range(4):
        ts(R("pa", e, 512, 4), rw[e // 2], hi2[e // 2], OP.add, p2[e // 2], OP.is_equal)
    qq("pa", 0, 128, R("pa", 0, 512))
    mq(6, "pa", 0, "pm", 0)
    cp(R("l18"), bank(6, 18))
    qq("q0", 0, 256, R("xt"))
    act(R("sqa"), R("rowb"), AF.Square, bias=col(4), scale=-1.0)
    for e in range(4):
        act(R("pa", 512 + e, 1024, 4), R("sqa"), AF.Relu, bias=1.0, scale=-1.0)
    qq("pa", 128, 128, R("pa", 512, 1024))
    ts(R("lo", 0, 1), p2[0], 255.0, OP.add, hi2[0], OP.subtract)
    ts(R("lo", 1, 2), p2[1], hi2[1], OP.subtract)
    lin(R("P1", 514, 576, 4), gm, 64.0 * r)
    for h in range(2):
        a, g8 = 512 + 32 * h, R("gmt", 0, 24, 3)
        ts(R("wr", h, h + 1), p2[h], 257.0 + 255 * h - 64 * r, OP.is_ge, -512.0, OP.mult)
        if h == 0:
            lin(R("P1", a, a + 32, 4), g8, hi2[0])
        else:
            ts(R("P1", a, a + 32, 4), g8, hi2[1], OP.mult)
        lin(R("P1", a + 1, a + 32, 4), g8, R("lo", h, h + 1))
        lin(R("P1", a + 3, a + 32, 4), g8, R("wr", h, h + 1))
    qq("pm", 128, 128, R("P1", 64, 576))
    mq(7, "pa", 128, "pm", 128)
    ts(R("pl"), bank(7, 16, 112), 0.5, OP.mult)
    lin(R("plf"), bank(7, 16, 112), 0.5)
    act(R("posn"), ind(R("iob"), R("pl")))

    def pick(d, a, b, s, w0, w1, off, own=False):
        oc, os = R(d + "c", a, b), R(d + "s", a, b)
        if own:
            oc, os = (oc[0], [(d + "c", 0, 256, 1)]), (os[0], [(d + "s", 0, 256, 1)])
        cp(W32(oc), ind(W32(R(s + "c", w0, w1)), off))
        act(os, ind(R(s + "s", w0, w1), off))

    others = [d for d in range(1, 8)]
    far = [d for d in others if topo.die(T.cores[r ^ d]) != topo.die(core)]
    near = [d for d in others if d not in far]
    lanes = {}
    for k, l in enumerate((far, near)):
        for n, d in enumerate(l):
            e = topo.engines(core, T.cores[r ^ d])
            lanes[d] = [e[4 * n + k], e[4 * n + 2 + k]]

    def send(srcs, dsts, sem, regs):
        def call():
            tf = []
            for d in others:
                ad = topo.addr(T.cores[r ^ d])
                tf.append(RemoteDMATransfer(dst_ids=[DstId(rid=ad[0], pnc=ad[1])], dma_engine_mask=sum(1 << e for e in lanes[d]),
                                            remote_sem=T.sem[sem], src=srcs(blk[r ^ d]), dst=dsts(blk[r ^ d])))
            g.remote_dma_fused(tf, local_sem=T.sem.loc)
            cnt["loc"] = cnt.get("loc", 0) + 14
        me = issue("p", call, [(b, lo, hi, 1) for b, lo, hi in regs], [], None, 1)
        group.setdefault(sem, []).append(len(ops))
        ops.append(["a", None, [me], sem, 14])

    def arrive(sem, b, lo, hi):
        acc.setdefault(b, []).append((lo, hi, 1, True, group[sem][0]))

    def send_w(b, sem):
        bc, bs = b + "c", b + "s"
        send(lambda q: T[bc][:, 256 + 32 * q:288 + 32 * q].bitcast(dt.uint8), lambda q: T[bc][:, 32 * q:32 * q + 32].bitcast(dt.uint8),
             sem, [(bc, 256, 512)])
        send(lambda q: T[bs][:, 256 + 32 * q:288 + 32 * q], lambda q: T[bs][:, 32 * q:32 * q + 32], sem, [(bs, 256, 512)])

    def diagonal(o, x, i, off):
        tt(x, ind(i, off), R("dm"), OP.mult)
        scan(o, R("rs16"), x, OP.mult, OP.add)

    def decode(s, a, start, stop):
        for b in range(4):
            mq(b, "eq", 128 * b, s, a, 256, start, stop)

    def local_scores(t, b, m, m0):
        for h in range(2):
            mq(4 + h, b, 256 + 128 * h, m, m0, 256)
            lin(R("gs", 256 * h, 256 * h + 256), bank(4 + h, 256))
        for h in range(2):
            tt(R("gg", 34 * h + 1, 34 * h + 33), ind(R("gs", 256 * h, 256 * h + 256), R("xp" if t else "xo", 2 * h, 2 * h + 2)), R("dm", 0, 32), OP.mult)
        scan(R("sc"), R("rs17"), R("gg"), OP.mult, OP.add)
        s1, s0 = R("sc", 16, 68, 34), R("sc", 33, 68, 34)
        ma, mx = "ma%d" % t, "mx%d" % t
        tt(R("m%d" % t), s0, s1, OP.max)
        for h in range(2):
            ts(R(ma, 4 * h, 4 * h + 4), R("msk", 4 * h, 4 * h + 4), R("sc", 16 + 34 * h, 17 + 34 * h), OP.add, R("sc", 33 + 34 * h, 34 + 34 * h), OP.max)
        send(lambda q: T[ma][:, q:q + 1], lambda q: T[mx][:, q:q + 1], "e%d" % t, [(ma, 0, 8)])
        o = 32 * (lb % 4)
        rest = [(0, o), (o + 32, 128)] if 0 < o < 96 else [(32 - o // 3, 64), (64, 128 - o // 3)]
        for i, (lo, hi, to) in enumerate([(o, o + 16, o + 16), (o + 16, o + 32, o)] + [(lo, hi, lo) for lo, hi in rest]):
            dma("y", "lm%d" % t, (T[mx][to:to + hi - lo, lb:lb + 1], [(mx, 0, 8, 1)] if i == 0 else []), (T[ma][lo:hi, lb:lb + 1], [(ma, 0, 8, 1)]))
        for h in range(2):
            ts(R("sm", h, h + 1), R("sc", 33 + 34 * h, 34 + 34 * h), R("sc", 16 + 34 * h, 17 + 34 * h), OP.is_ge, 0.5, OP.subtract)

    def ahead(t, b):
        sel, ct, ns = "sel%d" % t, "ct%d" % t, "ns%d" % t
        decode(b, 256, True, True)
        for e in range(4):
            lin(R("dh", 256 * e, 256 * e + 256), bank(e, 256), 0.5)
            lin(R("dk", 256 * e, 256 * e + 256), R("dh", 256 * e, 256 * e + 256))
        decode(b, 256, True, False)
        for h in range(2):
            lin(R("st", h, 10, 2), R("dif", h, 10, 2), R("sm", h, h + 1))
        tt(R(sel, 0, 10), R("st"), R("mid", 10, 20), OP.add)
        s = 2 * (1 - t)
        for h in range(2):
            ts(R(ct, 2 + h, 512, 4), R("rowb"), R(sel, 4 + s + h, 5 + s + h), OP.is_equal, BIG, OP.mult)
            lin(R(ns, 128 * h + 1, 128 * h + 128, 2), R("qm"), None, R(sel, s + h, s + h + 1))
        qq("cq", 128 * t, 128, R(ct))
        for h in range(2):
            relu(R("UC", 32 * h, 32 * h + 32), R("gx", 32 * h, 32 * h + 32), R("sm", h, h + 1))
        qq("uq", 128 * t, 128, R("UC"))
        mq(6, "cq", 256, "uq", 128 * t)
        ts(R("lp", 16 * t, 16 * t + 16), bank(6, 16), 1.0 / BIG, OP.mult)
        for h in range(2):
            for e in range(4):
                tt(R("ntl", 512 * h + e, 512 * h + 512, 4), ind(R("dh", 256 * e, 256 * e + 256), R("lp", 16 * t + 8 * h, 16 * t + 8 * h + 8)),
                   R("dk", 256 * e + 128 * h, 256 * e + 128 * h + 128), OP.add)
        qq(b, 512, 256, R("ntl"))

    def choose(t, b, u):
        mx, m = "mx%d" % t, "m%d" % t
        arrive("a%d" % t, b + "c", 0, 256)
        arrive("a%d" % t, b + "s", 0, 256)
        arrive("e%d" % t, mx, 0, 8)
        for h in range(2):
            mq(4 + h, b, 256 + 128 * h, b, 128 * h)
            tt(R("xd", 129 * h, 129 * h + 128), bank(4 + h, 128), R("idn"), OP.mult)
            total(R("sm", 16 + h, 17 + h), R("xd", 129 * h, 129 * h + 128 + t), R("jk", 130 * h, 130 * h + 128 + t))
            ts(R("sm", 18 + h, 19 + h), R(m, h, h + 1), R("sm", 16 + h, 17 + h), OP.is_ge, R("sel%d" % t, 8 + h, 9 + h), OP.mult)
            ts(R("ofx", 4 * h, 4 * h + 4), R(mx, 4 * h, 4 * h + 4), R("sm", 16 + h, 17 + h), OP.is_ge, col(11), OP.add)
            act(R("jq", 64 * h, 64 * h + 64), ind(R("dw"), R("ofx", 4 * h, 4 * h + 4)), AF.Relu, bias=R("sm", 18 + h, 19 + h),
                accum=R("sm", 20 + h, 21 + h))
            ts(u(h), R("ns%d" % t, 128 * h, 128 * h + 128), R("sm", 20 + h, 21 + h), OP.add, R("sm", 18 + h, 19 + h), OP.is_equal)
        decode(b, 0, False, True)
        for e in range(4):
            lin(R("ntn", e, 1024, 4), bank(e, 256), 0.5)
        qq(b, 768, 256, R("ntn"))

    def final_list(t, a):
        tt(R("z"), bank(7, 64, a), R("plx%d" % t), OP.add)
        scan(R("zs"), R("rs4", 0, 64), R("z"), OP.min, OP.max)
        cp(R("ln", 20 * t, 20 * t + 16), R("zs", 3, 64, 4))

    pick("b0", 256, 512, "q0", 0, 256, R("l18", 0, 16))
    send_w("b0", "a0")
    pick("b0", 32 * lb, 32 * lb + 32, "q0", 0, 256, R("l18", 16, 18), True)
    resets(R("rs8"), 2, 8)
    resets(R("rs16"), 4, 16)
    resets(R("rs17"), 4, 17)
    ts(R("dm"), R("j64"), col(5), OP.is_equal)
    for a in range(2):
        ts(R("o01", 16 * a, 16 * a + 16), nl[1 - a], -256.0 * r, OP.add)
    act(R("nr"), ind(R("iob"), R("o01")))
    tt(R("iv", 0, 16), bank(6, 16), gm, OP.mult)
    scan(R("iv", 16, 32), R("rs8"), R("iv", 0, 16), OP.mult, OP.add)
    inv = R("iv", 23, 32, 8)
    cp(R("of4", 0, 4, 2), inv)
    ts(R("of4", 1, 4, 2), inv, 256.0, OP.add)
    diagonal(R("xi", 0, 64), R("xg"), R("nr"), R("of4"))
    cp(R("xo"), R("xi", 15, 64, 16))
    ts(R("msk"), R("d8"), col(2), OP.not_equal, 2e29, OP.mult)
    for h in range(2):
        fill(R("gg", 34 * h, 34 * h + 34, 33), 0.0)
    local_scores(0, "b0", "q0", 0)
    cp(R("xi", 128, 130), inv)
    ts(R("xi", 130, 132), R("xi", 128, 130), 240, OP.bitwise_and)
    ts(R("xi", 132, 134), R("xi", 128, 130), 15, OP.bitwise_and)
    cp(R("hv"), R("xi", 130, 134))
    for h in range(2):
        lin(R("ns1", 128 * h, 128 * h + 128, 2), R("qn"), None, R("hv", h, h + 1))
        ts(R("ct1", h, 512, 4), R("rowb"), R("hv", 2 + h, 3 + h), OP.is_equal, BIG, OP.mult)
    diagonal(R("xi", 64, 128), R("xg2"), R("posn"), R("xo"))
    cp(R("xp"), R("xi", 79, 128, 16))
    ts(R("xi", 136, 144), R("xi", 15, 128, 16), 240, OP.bitwise_and)
    ts(R("xi", 144, 152), R("xi", 15, 128, 16), 15, OP.bitwise_and)
    cp(R("hl", 0, 16), R("xi", 136, 152))
    pfill(R("hl", 16, 20, 2), -4.0)
    pfill(R("hl", 17, 20, 2), -8.0)
    tt(R("dif"), R("hl", 1, 20, 2), R("hl", 0, 20, 2), OP.subtract)
    tt(R("mid", 0, 10), R("hl", 1, 20, 2), R("hl", 0, 20, 2), OP.add)
    lin(R("mid", 10, 20), R("mid", 0, 10), 0.5)
    pickout(R("idn"), R("ones"), 0, 1)
    resets(R("rs4"), 32, 4, R("tab", 2048, 2176), -1.0)
    ts(R("dw"), R("iob", 0, 32), col(11), OP.is_equal, 3.0, OP.mult)
    iota(R("qm"), [[-16, 16], [-4, 2], [-1, 2]], -3, 0)
    pfill(R("qm", 0, 64, 4), -500.0)
    for e in range(4):
        lin(R("gm4", e, 64, 4), gm, 2.0 if e % 2 else -2.0)
    lin(R("col2", 0, 1), col(0), 4.0, col(1))
    ts(R("cof"), R("c44"), R("col2", 0, 1), OP.add)
    tt(R("gx"), ind(R("hl", 0, 16), R("cof")), R("gm4"), OP.mult)
    c4 = (768.0 - BIG, 512.0 - 2 * BIG, 256.0, 512.0 - 2 * BIG)
    for k in range(4):
        iota(R("c4", k, 64, 4), [[16, 16]], int(c4[k]), 0)
        lin(R("plx1", k, 64, 4), R("plf"), None, c4[k])
    lin(R("plx0"), R("c4"), None, col(5))
    lin(R("gth"), gm, 512.0 - 1e6, 1e6)
    ts(R("oh"), R("rowb"), col(5), OP.is_equal, BIG, OP.mult)
    for e in range(4):
        lin(R("ct0", e, 512, 4), R("oh"))
    qq("cq", 256, 128, R("ct0"))
    for h in range(2):
        lin(R("ns0", 128 * h, 128 * h + 128, 2), R("qn"), None, col(6 + h))
    pickout(R("et"), R("one"), 3, 4)
    for b in range(4):
        qq("eq", 128 * b, 128, R("et", 3 - b, 515 - b))
    ahead(0, "b0")
    choose(0, "b0", lambda h: R("P1", 512 + h, 768, 2))
    qq("uq", 256, 128, R("P1", 256, 768))
    mq(7, "cq", 0, "uq", 256)
    final_list(0, 64)
    pick("b1", 256, 512, "b0", 0, 1024, R("ln", 0, 16))

    send_w("b1", "a1")
    for k in range(2):
        a = 4 * (2 * lb + 1 - k) + 3
        cp(R("ln", 16 + k, 17 + k), (T.zs[:, a:a + 1], [("zs", 0, 64, 1)]))
    pick("b1", 32 * lb, 32 * lb + 32, "b0", 0, 1024, R("ln", 16, 18), True)
    tt(R("fl", 0, 16), R("zs", 3, 64, 4), R("gth"), OP.is_ge)
    scan(R("fl", 16, 32), R("rs8"), R("fl", 0, 16), OP.mult, OP.add)
    tt(R("sm", 22, 24), R("sm", 18, 20), R("sm", 20, 22), OP.subtract)
    tt(R("sm", 24, 26), R("fl", 23, 32, 8), R("sm", 22, 24), OP.mult)
    for h in range(2):
        ts(R("gg", 34 * h, 34 * h + 34, 33), R("qn", 1, 4, 2), R("sm", 24 + h, 25 + h), OP.is_equal, -1e29, OP.mult)
    ts(R("xd", 128, 258, 129), R("sm", 24, 26), -3.0, OP.is_equal, -1e29, OP.mult)
    local_scores(1, "b1", "b1", 256)
    ts(R("sm", 26, 28), R("sm", 24, 26), -4.0, OP.is_le, 1.0, OP.add)
    pfill(R("U1", 0, 256), 0.0)
    for h in range(2):
        ts(R("U1", h, 256, 4), R("ns1", 128 * h, 128 * h + 128, 2), R("sm", 24 + h, 25 + h), OP.is_equal, R("sm", 26 + h, 27 + h), OP.mult)
    pfill(R("nlx", 2, 64, 4), -1.0)
    for k in range(3):
        lin(R("nlx", (3, 1, 0)[k], 64, 4), nl[k], None, -BIG if k == 2 else -2 * BIG)
    qq("qw", 0, 128, R("wt"))
    ahead(1, "b1")
    choose(1, "b1", lambda h: R("U1", 256 + h, 512, 2))
    qq("uq", 384, 128, R("U1"))
    mq(7, "cq", 128, "uq", 384)
    final_list(1, 64)
    for h in range(2):
        a, b = 128 * h, 128 * h + 128
        pick("oq", a, b, "b1", 0, 1024, R("ln", 20 + 8 * h, 28 + 8 * h))
        dma("y", "st0", (T.oc[:, 4 * a:4 * b], []), W8(R("oqc", a, b)))
        mq(4 + h, "qw", 0, "oq", a)
    for t in range(2):
        tt(R("zp", 64 * t, 64 * t + 64), bank(7, 64, 64 * t), R("nlx"), OP.add)
    scan(R("zq"), R("rs4"), R("zp"), OP.min, OP.max)
    issue("v", lambda: g.vector.transpose(T.tp[0:32, :], T.zq[0:32, 3:128:4]), R("zq")[1], R("tp")[1], "qv", 1)
    dma("y", "st0", (T.pr[:, :], []), (T.tp[0:32, 0:16], R("tp")[1]))
    for k in range(4):
        dma("s" if k % 2 else "y", "st0", (T.osc[4 * k:4 * k + 4, :], []), (T.oqs[32 * k:32 * k + 4, :], [("oqs", 0, 256, 1)]))
    for h in range(2):
        lin(R("ys", 128 * h, 128 * h + 128), bank(4 + h, 128))
        dma("y" if h == 0 else "s", "st0", (T.y[:, 128 * h:128 * h + 128], []), R("ys", 128 * h, 128 * h + 128))

    emit()
    cnt.update({"a0": 28, "a1": 28, "e0": 14, "e1": 14})
    for sem in sorted(cnt):
        g.wait_ge(T.sem[sem], cnt[sem])


def rank_program(g, core, T, topo):
    if T.rank_of(core) is not None:
        program(g, core, T, topo)
